import numpy as np
import ml_dtypes


def mxq(x, axis, fmt="e4m3"):
    dtype, down = {"e4m3": (ml_dtypes.float8_e4m3fn, 7), "e5m2": (ml_dtypes.float8_e5m2, 14)}[fmt]
    v = np.moveaxis(np.asarray(x, np.float32).astype(ml_dtypes.bfloat16).astype(np.float64), axis, -1)
    blocks = v.reshape(v.shape[:-1] + (-1, 32))
    amax = np.abs(blocks).max(-1, keepdims=True)
    byte = np.maximum(np.where(amax > 0, np.frexp(amax)[1] - 1 + 127, 0) - down, 1)
    scale = np.exp2(byte - 127.0)
    codes = (blocks / scale).astype(np.float32).astype(dtype).astype(np.float64)
    return np.moveaxis((codes * scale).reshape(v.shape), -1, axis)


WIDE = False


def mx_kscale(k):
    if not WIDE:
        return np.ones(k)
    levels = np.array([10, -10, 5, -5, 0])
    if k % 512:
        return np.exp2(np.random.permutation(np.resize(levels, k // 32))).repeat(32)
    a = np.empty((k // 512, 16))
    for p in range(k // 512):
        a[p, :8] = np.random.permutation(np.resize(levels, 8))
        for g in range(8):
            far = levels[np.abs(levels - a[p, g]) >= 10]
            a[p, g + 8] = far[np.random.randint(len(far))]
    return np.exp2(a.ravel()).repeat(32)


def f64(x):
    return np.asarray(x).astype(np.float64)


def striped(idx):
    return np.tile(idx.reshape(-1, 16).T, (8, 1)).astype(np.uint16)


def unstriped(offs):
    return offs[:16].T.reshape(-1).astype(np.int64)


E2M1 = np.array([0.0, 0.5, 1.0, 1.5, 2.0, 3.0, 4.0, 6.0, -0.0, -0.5, -1.0, -1.5, -2.0, -3.0, -4.0, -6.0])


def pack_weight(w, fmt):
    k, n = w.shape
    w = f64(np.asarray(w, np.float32).astype(ml_dtypes.bfloat16)).reshape(k // 32, 32, n)
    amax = np.abs(w).max(1)
    if fmt == "e4m3":
        byte = np.frexp(amax)[1] - 1 + 127 - 7
    else:
        mant, ex = np.frexp(amax / 6.0)
        byte = np.where(mant > 0.5, ex, ex - 1) + 127
    byte = np.clip(np.where(amax > 0, byte, 1), 1, 254)
    scaled = (w * np.exp2(127.0 - byte)[:, None, :]).reshape(k, n).astype(np.float32)
    by_word = np.ascontiguousarray(scaled.reshape(k // 512, 128, 4, n).transpose(0, 1, 3, 2))
    if fmt == "e4m3":
        words = by_word.astype(ml_dtypes.float8_e4m3fn).view(np.uint8)
    else:
        c = by_word.astype(ml_dtypes.float4_e2m1fn).view(np.uint8) & 0xF
        words = (c[..., 0::2] | (c[..., 1::2] << 4)).reshape(k // 512, 128, 2 * n)
    return np.ascontiguousarray(words), np.ascontiguousarray(byte.astype(np.uint8).reshape(k // 512, 16, n))


def unpack_weight(words, scales, fmt):
    g, _, n = scales.shape
    words = np.ascontiguousarray(words).reshape(g, 128, n, -1)
    if fmt == "e4m3":
        vals = words.view(ml_dtypes.float8_e4m3fn).astype(np.float64)
    else:
        nib = np.empty((g, 128, n, 4), np.uint8)
        nib[..., 0::2] = words & 0xF
        nib[..., 1::2] = words >> 4
        vals = E2M1[nib]
    vals = vals * np.repeat(np.exp2(scales.astype(np.float64) - 127.0), 8, axis=1)[..., None]
    return vals.transpose(0, 1, 3, 2).reshape(g * 512, n)


def gelu(v):
    return 0.5 * v * (1.0 + np.tanh(np.sqrt(2.0 / np.pi) * (v + 0.044715 * v**3)))


K, T, S, T2, S2, N = 1024, 4096, 1536, 1024, 512, 512

def setup_inputs():
    n = np.random.standard_normal
    s = mx_kscale(K)[:, None]
    u = mx_kscale(S)[:, None]
    tab_words, tab_scales = pack_weight(n((K, T)) * s / np.sqrt(K), "e4m3")
    tab2_words, tab2_scales = pack_weight(n((K, T2)) / s, "e4m3")
    g4_words, g4_scales = pack_weight(n((S, N)) / np.sqrt(S) / u, "e2m1")
    return {
        "tab_words": tab_words, "tab_scales": tab_scales,
        "offs": striped(np.random.permutation(T)[:S]),
        "tab2_words": tab2_words, "tab2_scales": tab2_scales,
        "offs2": striped(np.random.permutation(T2)[:S2]),
        "pw": (np.exp(0.3 * n(S)) * u[:, 0]).astype(np.float32),
        "x": (n((S, N)) / np.sqrt(S) / u).astype(np.float32),
        "g4_words": g4_words, "g4_scales": g4_scales,
    }

def reference(tab_words, tab_scales, offs, tab2_words, tab2_scales, offs2, pw, x, g4_words, g4_scales):
    v = unpack_weight(tab_words, tab_scales, "e4m3")[:, unstriped(offs)]
    v2 = unpack_weight(tab2_words, tab2_scales, "e4m3")[:, unstriped(offs2)]
    a = v.T @ v2
    h = np.square(np.maximum(a, 0.0)) * f64(pw)[:, None]
    hq = mxq(h, 0, "e4m3")
    xq = mxq(f64(x), 0, "e4m3")
    g4 = unpack_weight(g4_words, g4_scales, "e2m1")
    y = xq.T @ hq
    g = g4.T @ hq
    return y * (1.0 / (1.0 + np.exp(-g)))

@@ -1,0 +1,224 @@
+from contextlib import ExitStack
+
+import concourse.mybir as mybir
+
+F32 = mybir.dt.float32
+BF16 = mybir.dt.bfloat16
+I32 = mybir.dt.int32
+U32 = mybir.dt.uint32
+U16 = mybir.dt.uint16
+U8 = mybir.dt.uint8
+E4M3 = mybir.dt.float8_e4m3fn_x4
+E2M1 = mybir.dt.float4_e2m1fn_x4
+ALU = mybir.AluOpType
+ACT = mybir.ActivationFunctionType
+
+P = 128
+K, T, S, T2, S2, N = 1024, 4096, 1536, 1024, 512, 512
+PACK = 4
+PASS = P * PACK
+KP = K // PASS
+NB = S // PASS
+JC = S2 // P
+NT = N // P
+LIST_COLS = PASS // 16
+U_STEP = P + 1
+
+FLOPS = 2 * K * S * S2 + 2 * 2 * S * N * S2
+
+
+def tile_list_region_patch_pool_kernel(
+    tc, tab_words, tab_scales, offs, tab2_words, tab2_scales, offs2, pw, x, g4_words, g4_scales, out
+):
+    nc = tc.nc
+    with ExitStack() as ctx:
+        keep = ctx.enter_context(tc.tile_pool(name="keep", bufs=1))
+        ring = ctx.enter_context(tc.tile_pool(name="ring", bufs=3))
+        psum = ctx.enter_context(tc.psum_pool(name="psum", bufs=1))
+
+        idx = keep.tile([P, S // 16], U16, name="idx")
+        idx2 = keep.tile([P, S2 // 16], U16, name="idx2")
+        v_tab = [keep.tile([P, T], I32, name=f"v_tab{a}", align_bytes=64) for a in range(KP)]
+        v2_tab = [keep.tile([P, T2], I32, name=f"v2_tab{a}", align_bytes=64) for a in range(KP)]
+        v_tab_sc = keep.tile([P, T // 4], I32, name="v_tab_sc", align_bytes=64)
+        v2_tab_sc = keep.tile([P, T2 // 4], I32, name="v2_tab_sc", align_bytes=64)
+        g4_w = keep.tile([P, NB, 2 * N], U8, name="g4_w", align_bytes=64)
+        g4_sc = keep.tile([P, NB, N // 4], I32, name="g4_sc", align_bytes=64)
+        pw_sb = keep.tile([P, NB, 8], F32, name="pw_sb")
+        x_raw = [keep.tile([P, PACK, N], F32, name=f"x_raw{b}", align_bytes=64) for b in range(NB)]
+        warm = keep.tile([P, 8], F32, name="warm")
+
+        nc.vector.memset(v_tab_sc[:], 0)
+        nc.vector.memset(v2_tab_sc[:], 0)
+        nc.vector.memset(g4_sc[:], 0)
+        nc.vector.memset(warm[:, 0:1], 0.0)
+        nc.scalar.activation(warm[:, 1:2], warm[:, 0:1], ACT.Sigmoid)
+
+        def words_of(table, a):
+            return table[a].rearrange("p t i -> p (t i)").bitcast(I32)
+
+        def load_x(b):
+            nc.sync.dma_start(x_raw[b][:], x[b * PASS : (b + 1) * PASS, :].rearrange("(p t) n -> p t n", t=PACK))
+
+        nc.sync.dma_start(idx2[:], offs2)
+        for a in range(KP):
+            nc.sync.dma_start(v2_tab[a][:], words_of(tab2_words, a))
+        nc.sync.dma_start(idx[:], offs)
+        for q in range(4):
+            nc.sync.dma_start(v_tab_sc[32 * q : 32 * q + 8, :], tab_scales[:, 4 * q : 4 * q + 4, :].bitcast(I32))
+        nc.sync.dma_start(v_tab[0][:], words_of(tab_words, 0))
+        for q in range(4):
+            nc.sync.dma_start(v2_tab_sc[32 * q + 8 : 32 * q + 16, :], tab2_scales[:, 4 * q : 4 * q + 4, :].bitcast(I32))
+        nc.sync.dma_start(v_tab[1][:], words_of(tab_words, 1))
+        nc.sync.dma_start(pw_sb[:, :, 0:PACK], pw.rearrange("(b p t) -> p b t", p=P, t=PACK))
+        load_x(0)
+        load_x(1)
+        for q in range(4):
+            nc.sync.dma_start(
+                g4_sc[32 * q : 32 * q + 4, :, :],
+                g4_scales[:, 4 * q : 4 * q + 4, :].rearrange("a r c -> r a c").bitcast(I32),
+            )
+        nc.sync.dma_start(g4_w[:].bitcast(I32), g4_words.rearrange("a p c -> p a c").bitcast(I32))
+        load_x(2)
+
+        v2_w = [keep.tile([P, S2], U32, name=f"v2_w{a}", align_bytes=64) for a in range(KP)]
+        v2_sc = keep.tile([P, S2], U8, name="v2_sc", align_bytes=64)
+        for a in range(KP):
+            nc.vector.tensor_copy(v2_w[a][:], v2_tab[a][:].bitcast(U32).indirect(idx2[:]))
+
+        v_w = [[keep.tile([P, PASS], U32, name=f"v_w{a}_{b}", align_bytes=64) for b in range(NB)] for a in range(KP)]
+        v_sc_list = keep.tile([P, S], U8, name="v_sc_list", align_bytes=64)
+        v_sc = keep.tile([P, S], U8, name="v_sc", align_bytes=64)
+
+        def entries(b):
+            return idx[:, b * LIST_COLS : (b + 1) * LIST_COLS]
+
+        def gather_words(a, b):
+            nc.vector.tensor_copy(
+                v_w[a][b][:].rearrange("p (t m) -> p m t", t=PACK), v_tab[a][:].bitcast(U32).indirect(entries(b))
+            )
+
+        for b in range(NB):
+            nc.vector.tensor_copy(v_sc_list[:, b * PASS : (b + 1) * PASS], v_tab_sc[:].bitcast(U8).indirect(entries(b)))
+        nc.vector.tensor_copy(
+            v_sc[:].rearrange("p (b t m) -> p b t m", b=NB, t=PACK),
+            v_sc_list[:].rearrange("p (b m t) -> p b t m", b=NB, t=PACK),
+        )
+        for b in range(NB):
+            gather_words(0, b)
+        nc.vector.tensor_copy(v2_sc[:], v2_tab_sc[:].bitcast(U8).indirect(idx2[:]))
+
+        x_bf = [keep.tile([P, N * PACK], BF16, name=f"x_bf{b}", align_bytes=64) for b in range(NB)]
+        x_w = [keep.tile([P, N], U32, name=f"x_w{b}", align_bytes=64) for b in range(NB)]
+        x_sc = [keep.tile([P, N], U8, name=f"x_sc{b}", align_bytes=64) for b in range(NB)]
+        h_bf = [keep.tile([P, S2 * PACK], BF16, name=f"h_bf{b}", align_bytes=64) for b in range(NB)]
+        h_w = [keep.tile([P, S2], U32, name=f"h_w{b}", align_bytes=64) for b in range(NB)]
+        h_sc = [keep.tile([P, S2], U8, name=f"h_sc{b}", align_bytes=64) for b in range(NB)]
+
+        def cast_x(copy, b, c0, c1):
+            copy(
+                x_bf[b][:, c0 * PASS : c1 * PASS].rearrange("p (c i t) -> p c t i", i=4, t=PACK),
+                x_raw[b][:, :, c0 * P : c1 * P].rearrange("p t (c i) -> p c t i", i=4),
+            )
+
+        def quantize_x(b):
+            nc.vector.quantize_mx(out=x_w[b][:].bitcast(E4M3), scales=x_sc[b][:], in_=x_bf[b][:])
+
+        def quantize_h(b, c0, c1):
+            nc.vector.quantize_mx(
+                out=h_w[b][:, c0 * P : c1 * P].bitcast(E4M3),
+                scales=h_sc[b][:, c0 * P : c1 * P],
+                in_=h_bf[b][:, c0 * PASS : c1 * PASS],
+            )
+
+        def scores(b, c):
+            bank = psum.tile([P, PACK, P], F32, name="bank", tag="turn", bufs=4)
+            cols = slice(c * P, (c + 1) * P)
+            for t in range(PACK):
+                for a in range(KP):
+                    nc.tensor.matmul_mx(
+                        out=bank[:, t, :],
+                        lhsT=v_w[a][b][:, t * P : (t + 1) * P].bitcast(E4M3),
+                        lhsT_scale=v_sc[4 * a :, b * PASS + t * P : b * PASS + (t + 1) * P],
+                        rhs=v2_w[a][:, cols].bitcast(E4M3),
+                        rhs_scale=v2_sc[8 + 4 * a :, cols],
+                        start=(a == 0),
+                        stop=(a == KP - 1),
+                    )
+            weighted = ring.tile([P, PACK, U_STEP], F32, name="weighted")
+            for t in range(PACK):
+                nc.scalar.activation(weighted[:, t, 0:P], bank[:, t, :], ACT.Copy, scale=pw_sb[:, b, t : t + 1])
+            nc.vector.scalar_tensor_tensor(
+                out=h_bf[b][:, c * PASS : (c + 1) * PASS].rearrange("p (j t) -> p j t", t=PACK),
+                in0=bank[:].rearrange("p t j -> p j t"),
+                scalar=0.0,
+                in1=weighted[:, :, 0:P].rearrange("p t j -> p j t"),
+                op0=ALU.max,
+                op1=ALU.mult,
+            )
+
+        def gate_pass(acc, n, b):
+            nc.tensor.matmul_mx(
+                out=acc[:],
+                lhsT=g4_w[:, b, 2 * n * P : 2 * (n + 1) * P].bitcast(E2M1),
+                lhsT_scale=g4_sc[:, b, :].bitcast(U8)[:, n * P : (n + 1) * P],
+                rhs=h_w[b][:].bitcast(E4M3),
+                rhs_scale=h_sc[b][:],
+                start=(b == 0),
+                stop=(b == NB - 1),
+            )
+
+        def value_pass(acc, n, b):
+            nc.tensor.matmul_mx(
+                out=acc[:],
+                lhsT=x_w[b][:, n * P : (n + 1) * P].bitcast(E4M3),
+                lhsT_scale=x_sc[b][:, n * P : (n + 1) * P],
+                rhs=h_w[b][:].bitcast(E4M3),
+                rhs_scale=h_sc[b][:],
+                start=(b == 0),
+                stop=(b == NB - 1),
+            )
+
+        early = NT // 2
+        g_acc = [psum.tile([P, S2], F32, name=f"g_acc{n}") for n in range(early)]
+        y_acc = [psum.tile([P, S2], F32, name=f"y_acc{n}") for n in range(early)]
+
+        gather_words(1, 0)
+        for b in range(NB):
+            if b + 1 < NB:
+                gather_words(1, b + 1)
+            for c in range(JC):
+                scores(b, c)
+                if b < NB - 1 or c == 0:
+                    cast_x(nc.scalar.copy, b, c, c + 1)
+                if b == NB - 1 and c == 0:
+                    cast_x(nc.vector.tensor_copy, b, 1, JC)
+                if c == 0 and b > 0:
+                    quantize_h(b - 1, 0, JC)
+                if c == 1 and b > 0:
+                    quantize_x(b - 1)
+                    for n in range(early):
+                        gate_pass(g_acc[n], n, b - 1)
+                        value_pass(y_acc[n], n, b - 1)
+                if b == NB - 1 and c == 2:
+                    quantize_x(b)
+                if b == NB - 1 and c > 0:
+                    quantize_h(b, c - 1, c)
+        quantize_h(NB - 1, JC - 1, JC)
+
+        for n in range(early, NT):
+            g_acc.append(psum.tile([P, S2], F32, name=f"g_acc{n}", tag="turn", bufs=4))
+            y_acc.append(psum.tile([P, S2], F32, name=f"y_acc{n}", tag="turn", bufs=4))
+            for b in range(NB - 1):
+                gate_pass(g_acc[n], n, b)
+            for b in range(NB - 1):
+                value_pass(y_acc[n], n, b)
+
+        for n in range(NT):
+            gate_pass(g_acc[n], n, NB - 1)
+            value_pass(y_acc[n], n, NB - 1)
+            gate = keep.tile([P, S2], F32, name=f"gate{n}")
+            nc.scalar.activation(gate[:], g_acc[n][:], ACT.Sigmoid)
+            res = keep.tile([P, S2], F32, name=f"res{n}")
+            nc.vector.tensor_tensor(res[:], y_acc[n][:], gate[:], ALU.mult)
+            nc.sync.dma_start(out[n * P : (n + 1) * P, :], res[:])

@@ -22,7 +22,7 @@ NB = S // PASS
 JC = S2 // P
 NT = N // P
 LIST_COLS = PASS // 16
-U_STEP = P + 1
+U_STEP = P
 
 FLOPS = 2 * K * S * S2 + 2 * 2 * S * N * S2
 
@@ -64,21 +64,21 @@ def tile_list_region_patch_pool_kernel(
         for a in range(KP):
             nc.sync.dma_start(v2_tab[a][:], words_of(tab2_words, a))
         nc.sync.dma_start(idx[:], offs)
+        nc.sync.dma_start(pw_sb[:, :, 0:PACK], pw.rearrange("(b p t) -> p b t", p=P, t=PACK))
         for q in range(4):
             nc.sync.dma_start(v_tab_sc[32 * q : 32 * q + 8, :], tab_scales[:, 4 * q : 4 * q + 4, :].bitcast(I32))
         nc.sync.dma_start(v_tab[0][:], words_of(tab_words, 0))
         for q in range(4):
             nc.sync.dma_start(v2_tab_sc[32 * q + 8 : 32 * q + 16, :], tab2_scales[:, 4 * q : 4 * q + 4, :].bitcast(I32))
         nc.sync.dma_start(v_tab[1][:], words_of(tab_words, 1))
-        nc.sync.dma_start(pw_sb[:, :, 0:PACK], pw.rearrange("(b p t) -> p b t", p=P, t=PACK))
         load_x(0)
-        load_x(1)
         for q in range(4):
             nc.sync.dma_start(
                 g4_sc[32 * q : 32 * q + 4, :, :],
                 g4_scales[:, 4 * q : 4 * q + 4, :].rearrange("a r c -> r a c").bitcast(I32),
             )
         nc.sync.dma_start(g4_w[:].bitcast(I32), g4_words.rearrange("a p c -> p a c").bitcast(I32))
+        load_x(1)
         load_x(2)
 
         v2_w = [keep.tile([P, S2], U32, name=f"v2_w{a}", align_bytes=64) for a in range(KP)]
@@ -117,8 +117,8 @@ def tile_list_region_patch_pool_kernel(
 
         def cast_x(copy, b, c0, c1):
             copy(
-                x_bf[b][:, c0 * PASS : c1 * PASS].rearrange("p (c i t) -> p c t i", i=4, t=PACK),
-                x_raw[b][:, :, c0 * P : c1 * P].rearrange("p t (c i) -> p c t i", i=4),
+                x_bf[b][:, c0 * PASS : c1 * PASS].rearrange("p (c i t) -> p c t i", i=2, t=PACK),
+                x_raw[b][:, :, c0 * P : c1 * P].rearrange("p t (c i) -> p c t i", i=2),
             )
 
         def quantize_x(b):
@@ -189,10 +189,10 @@ def tile_list_region_patch_pool_kernel(
                 gather_words(1, b + 1)
             for c in range(JC):
                 scores(b, c)
-                if b < NB - 1 or c == 0:
+                if b < NB - 1:
                     cast_x(nc.scalar.copy, b, c, c + 1)
-                if b == NB - 1 and c == 0:
-                    cast_x(nc.vector.tensor_copy, b, 1, JC)
+                elif c < 2:
+                    cast_x(nc.scalar.copy, b, 2 * c, 2 * c + 2)
                 if c == 0 and b > 0:
                     quantize_h(b - 1, 0, JC)
                 if c == 1 and b > 0:

@@ -48,8 +48,8 @@ def tile_list_region_patch_pool_kernel(
         x_raw = [keep.tile([P, PACK, N], F32, name=f"x_raw{b}", align_bytes=64) for b in range(NB)]
         warm = keep.tile([P, 8], F32, name="warm")
 
-        nc.vector.memset(v_tab_sc[:], 0)
         nc.vector.memset(v2_tab_sc[:], 0)
+        nc.gpsimd.memset(v_tab_sc[:], 0)
         nc.vector.memset(g4_sc[:], 0)
         nc.vector.memset(warm[:, 0:1], 0.0)
         nc.scalar.activation(warm[:, 1:2], warm[:, 0:1], ACT.Sigmoid)
@@ -63,28 +63,30 @@ def tile_list_region_patch_pool_kernel(
         nc.sync.dma_start(idx2[:], offs2)
         for a in range(KP):
             nc.sync.dma_start(v2_tab[a][:], words_of(tab2_words, a))
-        nc.sync.dma_start(idx[:], offs)
-        nc.sync.dma_start(pw_sb[:, :, 0:PACK], pw.rearrange("(b p t) -> p b t", p=P, t=PACK))
-        for q in range(4):
-            nc.sync.dma_start(v_tab_sc[32 * q : 32 * q + 8, :], tab_scales[:, 4 * q : 4 * q + 4, :].bitcast(I32))
-        nc.sync.dma_start(v_tab[0][:], words_of(tab_words, 0))
         for q in range(4):
             nc.sync.dma_start(v2_tab_sc[32 * q + 8 : 32 * q + 16, :], tab2_scales[:, 4 * q : 4 * q + 4, :].bitcast(I32))
-        nc.sync.dma_start(v_tab[1][:], words_of(tab_words, 1))
+        nc.sync.dma_start(idx[:], offs)
+        for q in range(4):
+            queue = nc.gpsimd if q % 2 else nc.sync
+            queue.dma_start(v_tab_sc[32 * q : 32 * q + 8, :], tab_scales[:, 4 * q : 4 * q + 4, :].bitcast(I32))
+        nc.sync.dma_start(v_tab[0][:], words_of(tab_words, 0))
+        nc.sync.dma_start(pw_sb[:, :, 0:PACK], pw.rearrange("(b p t) -> p b t", p=P, t=PACK))
         load_x(0)
+        nc.sync.dma_start(v_tab[1][:], words_of(tab_words, 1))
+        load_x(1)
         for q in range(4):
             nc.sync.dma_start(
                 g4_sc[32 * q : 32 * q + 4, :, :],
                 g4_scales[:, 4 * q : 4 * q + 4, :].rearrange("a r c -> r a c").bitcast(I32),
             )
         nc.sync.dma_start(g4_w[:].bitcast(I32), g4_words.rearrange("a p c -> p a c").bitcast(I32))
-        load_x(1)
         load_x(2)
 
         v2_w = [keep.tile([P, S2], U32, name=f"v2_w{a}", align_bytes=64) for a in range(KP)]
         v2_sc = keep.tile([P, S2], U8, name="v2_sc", align_bytes=64)
         for a in range(KP):
             nc.vector.tensor_copy(v2_w[a][:], v2_tab[a][:].bitcast(U32).indirect(idx2[:]))
+        nc.vector.tensor_copy(v2_sc[:], v2_tab_sc[:].bitcast(U8).indirect(idx2[:]))
 
         v_w = [[keep.tile([P, PASS], U32, name=f"v_w{a}_{b}", align_bytes=64) for b in range(NB)] for a in range(KP)]
         v_sc_list = keep.tile([P, S], U8, name="v_sc_list", align_bytes=64)
@@ -106,7 +108,6 @@ def tile_list_region_patch_pool_kernel(
         )
         for b in range(NB):
             gather_words(0, b)
-        nc.vector.tensor_copy(v2_sc[:], v2_tab_sc[:].bitcast(U8).indirect(idx2[:]))
 
         x_bf = [keep.tile([P, N * PACK], BF16, name=f"x_bf{b}", align_bytes=64) for b in range(NB)]
         x_w = [keep.tile([P, N], U32, name=f"x_w{b}", align_bytes=64) for b in range(NB)]
@@ -183,6 +184,8 @@ def tile_list_region_patch_pool_kernel(
         g_acc = [psum.tile([P, S2], F32, name=f"g_acc{n}") for n in range(early)]
         y_acc = [psum.tile([P, S2], F32, name=f"y_acc{n}") for n in range(early)]
 
+        for c in range(JC):
+            cast_x(nc.scalar.copy, 0, c, c + 1)
         gather_words(1, 0)
         for b in range(NB):
             if b + 1 < NB:
@@ -190,9 +193,7 @@ def tile_list_region_patch_pool_kernel(
             for c in range(JC):
                 scores(b, c)
                 if b < NB - 1:
-                    cast_x(nc.scalar.copy, b, c, c + 1)
-                elif c < 2:
-                    cast_x(nc.scalar.copy, b, 2 * c, 2 * c + 2)
+                    cast_x(nc.scalar.copy, b + 1, c, c + 1)
                 if c == 0 and b > 0:
                     quantize_h(b - 1, 0, JC)
                 if c == 1 and b > 0:
@@ -200,11 +201,10 @@ def tile_list_region_patch_pool_kernel(
                     for n in range(early):
                         gate_pass(g_acc[n], n, b - 1)
                         value_pass(y_acc[n], n, b - 1)
-                if b == NB - 1 and c == 2:
-                    quantize_x(b)
                 if b == NB - 1 and c > 0:
                     quantize_h(b, c - 1, c)
         quantize_h(NB - 1, JC - 1, JC)
+        quantize_x(NB - 1)
 
         for n in range(early, NT):
             g_acc.append(psum.tile([P, S2], F32, name=f"g_acc{n}", tag="turn", bufs=4))
@@ -214,11 +214,16 @@ def tile_list_region_patch_pool_kernel(
             for b in range(NB - 1):
                 value_pass(y_acc[n], n, b)
 
+        gate_pass(g_acc[0], 0, NB - 1)
         for n in range(NT):
-            gate_pass(g_acc[n], n, NB - 1)
+            if n + 1 < NT:
+                gate_pass(g_acc[n + 1], n + 1, NB - 1)
             value_pass(y_acc[n], n, NB - 1)
             gate = keep.tile([P, S2], F32, name=f"gate{n}")
-            nc.scalar.activation(gate[:], g_acc[n][:], ACT.Sigmoid)
             res = keep.tile([P, S2], F32, name=f"res{n}")
-            nc.vector.tensor_tensor(res[:], y_acc[n][:], gate[:], ALU.mult)
+            pieces = 2 if n == 0 else 1
+            for h in range(pieces):
+                cols = slice(h * S2 // pieces, (h + 1) * S2 // pieces)
+                nc.scalar.activation(gate[:, cols], g_acc[n][:, cols], ACT.Sigmoid)
+                nc.vector.tensor_tensor(res[:, cols], y_acc[n][:, cols], gate[:, cols], ALU.mult)
             nc.sync.dma_start(out[n * P : (n + 1) * P, :], res[:])

@@ -22,7 +22,7 @@ NB = S // PASS
 JC = S2 // P
 NT = N // P
 LIST_COLS = PASS // 16
-U_STEP = P
+U_STEP = P + 1
 
 FLOPS = 2 * K * S * S2 + 2 * 2 * S * N * S2
 
@@ -71,8 +71,8 @@ def tile_list_region_patch_pool_kernel(
             queue.dma_start(v_tab_sc[32 * q : 32 * q + 8, :], tab_scales[:, 4 * q : 4 * q + 4, :].bitcast(I32))
         nc.sync.dma_start(v_tab[0][:], words_of(tab_words, 0))
         nc.sync.dma_start(pw_sb[:, :, 0:PACK], pw.rearrange("(b p t) -> p b t", p=P, t=PACK))
-        load_x(0)
         nc.sync.dma_start(v_tab[1][:], words_of(tab_words, 1))
+        load_x(0)
         load_x(1)
         for q in range(4):
             nc.sync.dma_start(
@@ -121,6 +121,18 @@ def tile_list_region_patch_pool_kernel(
                 x_bf[b][:, c0 * PASS : c1 * PASS].rearrange("p (c i t) -> p c t i", i=2, t=PACK),
                 x_raw[b][:, :, c0 * P : c1 * P].rearrange("p t (c i) -> p c t i", i=2),
             )
+
+        def cast_x_gpsimd(b, c):
+            for h in range(2):
+                j0 = c * P + h * P // 2
+                nc.gpsimd.tensor_scalar(
+                    x_bf[b][:, j0 * PACK : (j0 + P // 2) * PACK].rearrange("p (j t) -> p j t", t=PACK),
+                    x_raw[b][:, :, j0 : j0 + P // 2].rearrange("p t j -> p j t"),
+                    1.0,
+                    0.0,
+                    ALU.mult,
+                    ALU.add,
+                )
 
         def quantize_x(b):
             nc.vector.quantize_mx(out=x_w[b][:].bitcast(E4M3), scales=x_sc[b][:], in_=x_bf[b][:])
@@ -184,16 +196,16 @@ def tile_list_region_patch_pool_kernel(
         g_acc = [psum.tile([P, S2], F32, name=f"g_acc{n}") for n in range(early)]
         y_acc = [psum.tile([P, S2], F32, name=f"y_acc{n}") for n in range(early)]
 
-        for c in range(JC):
-            cast_x(nc.scalar.copy, 0, c, c + 1)
+        for b, c in [(1, 2), (1, 3), (2, 0), (2, 1), (2, 2), (2, 3)]:
+            cast_x_gpsimd(b, c)
         gather_words(1, 0)
         for b in range(NB):
             if b + 1 < NB:
                 gather_words(1, b + 1)
             for c in range(JC):
                 scores(b, c)
-                if b < NB - 1:
-                    cast_x(nc.scalar.copy, b + 1, c, c + 1)
+                if b == 0 or (b == 1 and c < 2):
+                    cast_x(nc.scalar.copy, b, c, c + 1)
                 if c == 0 and b > 0:
                     quantize_h(b - 1, 0, JC)
                 if c == 1 and b > 0:
@@ -221,9 +233,12 @@ def tile_list_region_patch_pool_kernel(
             value_pass(y_acc[n], n, NB - 1)
             gate = keep.tile([P, S2], F32, name=f"gate{n}")
             res = keep.tile([P, S2], F32, name=f"res{n}")
-            pieces = 2 if n == 0 else 1
+            pieces = 2 if n in (0, NT - 1) else 1
             for h in range(pieces):
                 cols = slice(h * S2 // pieces, (h + 1) * S2 // pieces)
                 nc.scalar.activation(gate[:, cols], g_acc[n][:, cols], ACT.Sigmoid)
                 nc.vector.tensor_tensor(res[:, cols], y_acc[n][:, cols], gate[:, cols], ALU.mult)
-            nc.sync.dma_start(out[n * P : (n + 1) * P, :], res[:])
+                if n == NT - 1:
+                    nc.sync.dma_start(out[n * P : (n + 1) * P, cols], res[:, cols])
+            if n < NT - 1:
+                nc.sync.dma_start(out[n * P : (n + 1) * P, :], res[:])

@@ -24,6 +24,20 @@ NT = N // P
 LIST_COLS = PASS // 16
 U_STEP = P + 1
 
+RING = 4
+G4POS = 2
+SBANK = [0, 1, 2, 3, 4, 5, 0, 1, 2, 3, 0, 1]
+ABANK = {"g": [6, 4, 2, 0], "y": [7, 5, 3, 1]}
+POOL = {
+    5: [(k, n, 0) for n in (0, 1) for k in "gy"],
+    9: [(k, n, 1) for n in (0, 1) for k in "gy"],
+    11: [(k, n, b) for n in (2, 3) for k in "gy" for b in (0, 1)],
+}
+QH = {4: [(0, 0, 4)], 8: [(1, 0, 4)], 9: [(2, 0, 1)], 10: [(2, 1, 2)], 11: [(2, 2, 3), (2, 3, 4)]}
+GCASTS = [(b, c) for b in (0, 1) for c in range(4)]
+SCASTS = {7: [(2, 0)], 8: [(2, 1)], 9: [(2, 2)], 10: [(2, 3)]}
+QX = {5: [0], 9: [1], 11: [2]}
+
 FLOPS = 2 * K * S * S2 + 2 * 2 * S * N * S2
 
 
@@ -33,7 +47,7 @@ def tile_list_region_patch_pool_kernel(
     nc = tc.nc
     with ExitStack() as ctx:
         keep = ctx.enter_context(tc.tile_pool(name="keep", bufs=1))
-        ring = ctx.enter_context(tc.tile_pool(name="ring", bufs=3))
+        ring = ctx.enter_context(tc.tile_pool(name="ring", bufs=RING))
         psum = ctx.enter_context(tc.psum_pool(name="psum", bufs=1))
 
         idx = keep.tile([P, S // 16], U16, name="idx")
@@ -72,15 +86,20 @@ def tile_list_region_patch_pool_kernel(
         nc.sync.dma_start(v_tab[0][:], words_of(tab_words, 0))
         nc.sync.dma_start(pw_sb[:, :, 0:PACK], pw.rearrange("(b p t) -> p b t", p=P, t=PACK))
         nc.sync.dma_start(v_tab[1][:], words_of(tab_words, 1))
-        load_x(0)
-        load_x(1)
-        for q in range(4):
-            nc.sync.dma_start(
-                g4_sc[32 * q : 32 * q + 4, :, :],
-                g4_scales[:, 4 * q : 4 * q + 4, :].rearrange("a r c -> r a c").bitcast(I32),
-            )
-        nc.sync.dma_start(g4_w[:].bitcast(I32), g4_words.rearrange("a p c -> p a c").bitcast(I32))
-        load_x(2)
+        def load_g4():
+            for q in range(4):
+                nc.sync.dma_start(
+                    g4_sc[32 * q : 32 * q + 4, :, :],
+                    g4_scales[:, 4 * q : 4 * q + 4, :].rearrange("a r c -> r a c").bitcast(I32),
+                )
+            nc.sync.dma_start(g4_w[:].bitcast(I32), g4_words.rearrange("a p c -> p a c").bitcast(I32))
+
+        for b in range(NB):
+            if b == G4POS:
+                load_g4()
+            load_x(b)
+        if G4POS == NB:
+            load_g4()
 
         v2_w = [keep.tile([P, S2], U32, name=f"v2_w{a}", align_bytes=64) for a in range(KP)]
         v2_sc = keep.tile([P, S2], U8, name="v2_sc", align_bytes=64)
@@ -103,8 +122,8 @@ def tile_list_region_patch_pool_kernel(
         for b in range(NB):
             nc.vector.tensor_copy(v_sc_list[:, b * PASS : (b + 1) * PASS], v_tab_sc[:].bitcast(U8).indirect(entries(b)))
         nc.vector.tensor_copy(
-            v_sc[:].rearrange("p (b t m) -> p b t m", b=NB, t=PACK),
-            v_sc_list[:].rearrange("p (b m t) -> p b t m", b=NB, t=PACK),
+            v_sc[:].rearrange("p (b t m) -> p t b m", b=NB, t=PACK),
+            v_sc_list[:].rearrange("p (b m t) -> p t b m", b=NB, t=PACK),
         )
         for b in range(NB):
             gather_words(0, b)
@@ -145,18 +164,18 @@ def tile_list_region_patch_pool_kernel(
             )
 
         def scores(b, c):
-            bank = psum.tile([P, PACK, P], F32, name="bank", tag="turn", bufs=4)
+            bank = psum.tile([P, PACK, P], F32, name="bank", tag=f"bank{SBANK[b * JC + c]}")
             cols = slice(c * P, (c + 1) * P)
-            for t in range(PACK):
-                for a in range(KP):
+            for a in range(KP):
+                for t in range(PACK):
                     nc.tensor.matmul_mx(
                         out=bank[:, t, :],
                         lhsT=v_w[a][b][:, t * P : (t + 1) * P].bitcast(E4M3),
                         lhsT_scale=v_sc[4 * a :, b * PASS + t * P : b * PASS + (t + 1) * P],
                         rhs=v2_w[a][:, cols].bitcast(E4M3),
                         rhs_scale=v2_sc[8 + 4 * a :, cols],
-                        start=(a == 0),
-                        stop=(a == KP - 1),
+                        start=(a == 0 and t == 0),
+                        stop=(a == KP - 1 and t == PACK - 1),
                     )
             weighted = ring.tile([P, PACK, U_STEP], F32, name="weighted")
             for t in range(PACK):
@@ -192,39 +211,29 @@ def tile_list_region_patch_pool_kernel(
                 stop=(b == NB - 1),
             )
 
-        early = NT // 2
-        g_acc = [psum.tile([P, S2], F32, name=f"g_acc{n}") for n in range(early)]
-        y_acc = [psum.tile([P, S2], F32, name=f"y_acc{n}") for n in range(early)]
+        g_acc, y_acc = {}, {}
 
-        for b, c in [(1, 2), (1, 3), (2, 0), (2, 1), (2, 2), (2, 3)]:
+        def pool(kind, n, b):
+            accs = g_acc if kind == "g" else y_acc
+            if b == 0:
+                accs[n] = psum.tile([P, S2], F32, name=f"{kind}_acc{n}", tag=f"bank{ABANK[kind][n]}")
+            (gate_pass if kind == "g" else value_pass)(accs[n], n, b)
+
+        for b, c in GCASTS:
             cast_x_gpsimd(b, c)
-        gather_words(1, 0)
         for b in range(NB):
-            if b + 1 < NB:
-                gather_words(1, b + 1)
-            for c in range(JC):
-                scores(b, c)
-                if b == 0 or (b == 1 and c < 2):
-                    cast_x(nc.scalar.copy, b, c, c + 1)
-                if c == 0 and b > 0:
-                    quantize_h(b - 1, 0, JC)
-                if c == 1 and b > 0:
-                    quantize_x(b - 1)
-                    for n in range(early):
-                        gate_pass(g_acc[n], n, b - 1)
-                        value_pass(y_acc[n], n, b - 1)
-                if b == NB - 1 and c > 0:
-                    quantize_h(b, c - 1, c)
-        quantize_h(NB - 1, JC - 1, JC)
-        quantize_x(NB - 1)
-
-        for n in range(early, NT):
-            g_acc.append(psum.tile([P, S2], F32, name=f"g_acc{n}", tag="turn", bufs=4))
-            y_acc.append(psum.tile([P, S2], F32, name=f"y_acc{n}", tag="turn", bufs=4))
-            for b in range(NB - 1):
-                gate_pass(g_acc[n], n, b)
-            for b in range(NB - 1):
-                value_pass(y_acc[n], n, b)
+            gather_words(1, b)
+        for k in range(NB * JC):
+            b, c = divmod(k, JC)
+            scores(b, c)
+            for qb, c0, c1 in QH.get(k, []):
+                quantize_h(qb, c0, c1)
+            for xb, xc in SCASTS.get(k, []):
+                cast_x(nc.scalar.copy, xb, xc, xc + 1)
+            for xb in QX.get(k, []):
+                quantize_x(xb)
+            for kind, n, pb in POOL.get(k, []):
+                pool(kind, n, pb)
 
         gate_pass(g_acc[0], 0, NB - 1)
         for n in range(NT):

@@ -26,17 +26,18 @@ U_STEP = P + 1
 
 RING = 4
 G4POS = 2
+XEARLY = 0
 SBANK = [0, 1, 2, 3, 4, 5, 0, 1, 2, 3, 0, 1]
 ABANK = {"g": [6, 4, 2, 0], "y": [7, 5, 3, 1]}
 POOL = {
     5: [(k, n, 0) for n in (0, 1) for k in "gy"],
     9: [(k, n, 1) for n in (0, 1) for k in "gy"],
-    11: [(k, n, b) for n in (2, 3) for k in "gy" for b in (0, 1)],
+    11: [(k, n, b) for k, n in (("g", 2), ("y", 2), ("g", 3)) for b in (0, 1)],
 }
 QH = {4: [(0, 0, 4)], 8: [(1, 0, 4)], 9: [(2, 0, 1)], 10: [(2, 1, 2)], 11: [(2, 2, 3), (2, 3, 4)]}
-GCASTS = [(b, c) for b in (0, 1) for c in range(4)]
-SCASTS = {7: [(2, 0)], 8: [(2, 1)], 9: [(2, 2)], 10: [(2, 3)]}
-QX = {5: [0], 9: [1], 11: [2]}
+SCASTS = {2: [(1, 0)], 3: [(1, 1)], 4: [(1, 2)], 5: [(1, 3)], 6: [(2, 0)], 7: [(2, 1)], 8: [(2, 2)], 9: [(2, 3)]}
+VCASTS = {0: [(0, 0, 4)]}
+QX = {2: [0], 8: [1], 10: [2]}
 
 FLOPS = 2 * K * S * S2 + 2 * 2 * S * N * S2
 
@@ -85,6 +86,8 @@ def tile_list_region_patch_pool_kernel(
             queue.dma_start(v_tab_sc[32 * q : 32 * q + 8, :], tab_scales[:, 4 * q : 4 * q + 4, :].bitcast(I32))
         nc.sync.dma_start(v_tab[0][:], words_of(tab_words, 0))
         nc.sync.dma_start(pw_sb[:, :, 0:PACK], pw.rearrange("(b p t) -> p b t", p=P, t=PACK))
+        if XEARLY:
+            load_x(0)
         nc.sync.dma_start(v_tab[1][:], words_of(tab_words, 1))
         def load_g4():
             for q in range(4):
@@ -94,7 +97,7 @@ def tile_list_region_patch_pool_kernel(
                 )
             nc.sync.dma_start(g4_w[:].bitcast(I32), g4_words.rearrange("a p c -> p a c").bitcast(I32))
 
-        for b in range(NB):
+        for b in range(XEARLY, NB):
             if b == G4POS:
                 load_g4()
             load_x(b)
@@ -137,21 +140,9 @@ def tile_list_region_patch_pool_kernel(
 
         def cast_x(copy, b, c0, c1):
             copy(
-                x_bf[b][:, c0 * PASS : c1 * PASS].rearrange("p (c i t) -> p c t i", i=2, t=PACK),
-                x_raw[b][:, :, c0 * P : c1 * P].rearrange("p t (c i) -> p c t i", i=2),
+                x_bf[b][:, c0 * PASS : c1 * PASS].rearrange("p (c i t) -> p c t i", i=4, t=PACK),
+                x_raw[b][:, :, c0 * P : c1 * P].rearrange("p t (c i) -> p c t i", i=4),
             )
-
-        def cast_x_gpsimd(b, c):
-            for h in range(2):
-                j0 = c * P + h * P // 2
-                nc.gpsimd.tensor_scalar(
-                    x_bf[b][:, j0 * PACK : (j0 + P // 2) * PACK].rearrange("p (j t) -> p j t", t=PACK),
-                    x_raw[b][:, :, j0 : j0 + P // 2].rearrange("p t j -> p j t"),
-                    1.0,
-                    0.0,
-                    ALU.mult,
-                    ALU.add,
-                )
 
         def quantize_x(b):
             nc.vector.quantize_mx(out=x_w[b][:].bitcast(E4M3), scales=x_sc[b][:], in_=x_bf[b][:])
@@ -219,8 +210,10 @@ def tile_list_region_patch_pool_kernel(
                 accs[n] = psum.tile([P, S2], F32, name=f"{kind}_acc{n}", tag=f"bank{ABANK[kind][n]}")
             (gate_pass if kind == "g" else value_pass)(accs[n], n, b)
 
-        for b, c in GCASTS:
-            cast_x_gpsimd(b, c)
+        for xb, xc in SCASTS.get(-1, []):
+            cast_x(nc.scalar.copy, xb, xc, xc + 1)
+        for xb in QX.get(-1, []):
+            quantize_x(xb)
         for b in range(NB):
             gather_words(1, b)
         for k in range(NB * JC):
@@ -230,15 +223,18 @@ def tile_list_region_patch_pool_kernel(
                 quantize_h(qb, c0, c1)
             for xb, xc in SCASTS.get(k, []):
                 cast_x(nc.scalar.copy, xb, xc, xc + 1)
+            for xb, xc0, xc1 in VCASTS.get(k, []):
+                cast_x(nc.vector.tensor_copy, xb, xc0, xc1)
             for xb in QX.get(k, []):
                 quantize_x(xb)
             for kind, n, pb in POOL.get(k, []):
                 pool(kind, n, pb)
 
-        gate_pass(g_acc[0], 0, NB - 1)
         for n in range(NT):
-            if n + 1 < NT:
-                gate_pass(g_acc[n + 1], n + 1, NB - 1)
+            gate_pass(g_acc[n], n, NB - 1)
+            if n == NT - 1:
+                for b in range(NB - 1):
+                    pool("y", n, b)
             value_pass(y_acc[n], n, NB - 1)
             gate = keep.tile([P, S2], F32, name=f"gate{n}")
             res = keep.tile([P, S2], F32, name=f"res{n}")

@@ -35,9 +35,9 @@ POOL = {
     11: [(k, n, b) for k, n in (("g", 2), ("y", 2), ("g", 3)) for b in (0, 1)],
 }
 QH = {4: [(0, 0, 4)], 8: [(1, 0, 4)], 9: [(2, 0, 1)], 10: [(2, 1, 2)], 11: [(2, 2, 3), (2, 3, 4)]}
-SCASTS = {2: [(1, 0)], 3: [(1, 1)], 4: [(1, 2)], 5: [(1, 3)], 6: [(2, 0)], 7: [(2, 1)], 8: [(2, 2)], 9: [(2, 3)]}
-VCASTS = {0: [(0, 0, 4)]}
-QX = {2: [0], 8: [1], 10: [2]}
+SCASTS = {-1: [(0, 0), (0, 1)], 1: [(0, 2)], 2: [(0, 3)], 6: [(2, 0)], 7: [(2, 1)], 8: [(2, 2)], 9: [(2, 3)]}
+VCASTS = {3: [(1, 0, 4)]}
+QX = {3: [0], 5: [1], 10: [2]}
 
 FLOPS = 2 * K * S * S2 + 2 * 2 * S * N * S2
 
@@ -60,7 +60,8 @@ def tile_list_region_patch_pool_kernel(
         g4_w = keep.tile([P, NB, 2 * N], U8, name="g4_w", align_bytes=64)
         g4_sc = keep.tile([P, NB, N // 4], I32, name="g4_sc", align_bytes=64)
         pw_sb = keep.tile([P, NB, 8], F32, name="pw_sb")
-        x_raw = [keep.tile([P, PACK, N], F32, name=f"x_raw{b}", align_bytes=64) for b in range(NB)]
+        x_raw = [keep.tile([P, PACK, N], F32, name=f"x_raw{b}", align_bytes=64) for b in range(1, NB)]
+        x_half = [keep.tile([P, PACK, N // 2], F32, name=f"x_half{h}", tag=f"x_half{h}", align_bytes=64) for h in range(2)]
         warm = keep.tile([P, 8], F32, name="warm")
 
         nc.vector.memset(v2_tab_sc[:], 0)
@@ -73,7 +74,12 @@ def tile_list_region_patch_pool_kernel(
             return table[a].rearrange("p t i -> p (t i)").bitcast(I32)
 
         def load_x(b):
-            nc.sync.dma_start(x_raw[b][:], x[b * PASS : (b + 1) * PASS, :].rearrange("(p t) n -> p t n", t=PACK))
+            rows = x[b * PASS : (b + 1) * PASS, :].rearrange("(p t) n -> p t n", t=PACK)
+            if b == 0:
+                for h in range(2):
+                    nc.sync.dma_start(x_half[h][:], rows[:, :, h * N // 2 : (h + 1) * N // 2])
+            else:
+                nc.sync.dma_start(x_raw[b - 1][:], rows)
 
         nc.sync.dma_start(idx2[:], offs2)
         for a in range(KP):
@@ -139,9 +145,13 @@ def tile_list_region_patch_pool_kernel(
         h_sc = [keep.tile([P, S2], U8, name=f"h_sc{b}", align_bytes=64) for b in range(NB)]
 
         def cast_x(copy, b, c0, c1):
+            if b == 0:
+                src = x_half[c0 // 2][:, :, (c0 % 2) * P : (c0 % 2 + c1 - c0) * P]
+            else:
+                src = x_raw[b - 1][:, :, c0 * P : c1 * P]
             copy(
                 x_bf[b][:, c0 * PASS : c1 * PASS].rearrange("p (c i t) -> p c t i", i=4, t=PACK),
-                x_raw[b][:, :, c0 * P : c1 * P].rearrange("p t (c i) -> p c t i", i=4),
+                src.rearrange("p t (c i) -> p c t i", i=4),
             )
 
         def quantize_x(b):
@@ -168,7 +178,10 @@ def tile_list_region_patch_pool_kernel(
                         start=(a == 0 and t == 0),
                         stop=(a == KP - 1 and t == PACK - 1),
                     )
-            weighted = ring.tile([P, PACK, U_STEP], F32, name="weighted")
+            if b == 0 and c == 0:
+                weighted = keep.tile([P, PACK, U_STEP], F32, name="weighted", tag="x_half0", align_bytes=64)
+            else:
+                weighted = ring.tile([P, PACK, U_STEP], F32, name="weighted")
             for t in range(PACK):
                 nc.scalar.activation(weighted[:, t, 0:P], bank[:, t, :], ACT.Copy, scale=pw_sb[:, b, t : t + 1])
             nc.vector.scalar_tensor_tensor(

@@ -36,8 +36,9 @@ POOL = {
 }
 QH = {4: [(0, 0, 4)], 8: [(1, 0, 4)], 9: [(2, 0, 1)], 10: [(2, 1, 2)], 11: [(2, 2, 3), (2, 3, 4)]}
 SCASTS = {-1: [(0, 0), (0, 1)], 1: [(0, 2)], 2: [(0, 3)], 6: [(2, 0)], 7: [(2, 1)], 8: [(2, 2)], 9: [(2, 3)]}
-VCASTS = {3: [(1, 0, 4)]}
-QX = {3: [0], 5: [1], 10: [2]}
+VCASTS = {}
+GW = 64
+QX = {3: [0], 9: [1], 10: [2]}
 
 FLOPS = 2 * K * S * S2 + 2 * 2 * S * N * S2
 
@@ -154,6 +155,17 @@ def tile_list_region_patch_pool_kernel(
                 src.rearrange("p t (c i) -> p c t i", i=4),
             )
 
+        def cast_x_gpsimd(b):
+            for j0 in range(0, N, GW):
+                nc.gpsimd.tensor_scalar(
+                    x_bf[b][:, j0 * PACK : (j0 + GW) * PACK].rearrange("p (j t) -> p j t", t=PACK),
+                    x_raw[b - 1][:, :, j0 : j0 + GW].rearrange("p t j -> p j t"),
+                    1.0,
+                    0.0,
+                    ALU.mult,
+                    ALU.add,
+                )
+
         def quantize_x(b):
             nc.vector.quantize_mx(out=x_w[b][:].bitcast(E4M3), scales=x_sc[b][:], in_=x_bf[b][:])
 
@@ -223,6 +235,7 @@ def tile_list_region_patch_pool_kernel(
                 accs[n] = psum.tile([P, S2], F32, name=f"{kind}_acc{n}", tag=f"bank{ABANK[kind][n]}")
             (gate_pass if kind == "g" else value_pass)(accs[n], n, b)
 
+        cast_x_gpsimd(1)
         for xb, xc in SCASTS.get(-1, []):
             cast_x(nc.scalar.copy, xb, xc, xc + 1)
         for xb in QX.get(-1, []):

@@ -63,13 +63,10 @@ def tile_list_region_patch_pool_kernel(
         pw_sb = keep.tile([P, NB, 8], F32, name="pw_sb")
         x_raw = [keep.tile([P, PACK, N], F32, name=f"x_raw{b}", align_bytes=64) for b in range(1, NB)]
         x_half = [keep.tile([P, PACK, N // 2], F32, name=f"x_half{h}", tag=f"x_half{h}", align_bytes=64) for h in range(2)]
-        warm = keep.tile([P, 8], F32, name="warm")
 
         nc.vector.memset(v2_tab_sc[:], 0)
         nc.gpsimd.memset(v_tab_sc[:], 0)
         nc.vector.memset(g4_sc[:], 0)
-        nc.vector.memset(warm[:, 0:1], 0.0)
-        nc.scalar.activation(warm[:, 1:2], warm[:, 0:1], ACT.Sigmoid)
 
         def words_of(table, a):
             return table[a].rearrange("p t i -> p (t i)").bitcast(I32)

@@ -80,16 +80,16 @@ def tile_list_region_patch_pool_kernel(
                 nc.sync.dma_start(x_raw[b - 1][:], rows)
 
         nc.sync.dma_start(idx2[:], offs2)
-        for a in range(KP):
-            nc.sync.dma_start(v2_tab[a][:], words_of(tab2_words, a))
+        nc.sync.dma_start(v2_tab[0][:], words_of(tab2_words, 0))
+        nc.sync.dma_start(idx[:], offs)
+        nc.sync.dma_start(v2_tab[1][:], words_of(tab2_words, 1))
         for q in range(4):
             nc.sync.dma_start(v2_tab_sc[32 * q + 8 : 32 * q + 16, :], tab2_scales[:, 4 * q : 4 * q + 4, :].bitcast(I32))
-        nc.sync.dma_start(idx[:], offs)
         for q in range(4):
             queue = nc.gpsimd if q % 2 else nc.sync
             queue.dma_start(v_tab_sc[32 * q : 32 * q + 8, :], tab_scales[:, 4 * q : 4 * q + 4, :].bitcast(I32))
-        nc.sync.dma_start(v_tab[0][:], words_of(tab_words, 0))
         nc.sync.dma_start(pw_sb[:, :, 0:PACK], pw.rearrange("(b p t) -> p b t", p=P, t=PACK))
+        nc.sync.dma_start(v_tab[0][:], words_of(tab_words, 0))
         if XEARLY:
             load_x(0)
         nc.sync.dma_start(v_tab[1][:], words_of(tab_words, 1))

@@ -25,20 +25,9 @@ LIST_COLS = PASS // 16
 U_STEP = P + 1
 
 RING = 4
-G4POS = 2
-XEARLY = 0
 SBANK = [0, 1, 2, 3, 4, 5, 0, 1, 2, 3, 0, 1]
-ABANK = {"g": [6, 4, 2, 0], "y": [7, 5, 3, 1]}
-POOL = {
-    5: [(k, n, 0) for n in (0, 1) for k in "gy"],
-    9: [(k, n, 1) for n in (0, 1) for k in "gy"],
-    11: [(k, n, b) for k, n in (("g", 2), ("y", 2), ("g", 3)) for b in (0, 1)],
-}
-QH = {4: [(0, 0, 4)], 8: [(1, 0, 4)], 9: [(2, 0, 1)], 10: [(2, 1, 2)], 11: [(2, 2, 3), (2, 3, 4)]}
-SCASTS = {-1: [(0, 0), (0, 1)], 1: [(0, 2)], 2: [(0, 3)], 6: [(2, 0)], 7: [(2, 1)], 8: [(2, 2)], 9: [(2, 3)]}
-VCASTS = {}
+ABANK = {"g": [6, 7, 2, 0], "y": [4, 5, 3, 1]}
 GW = 64
-QX = {3: [0], 9: [1], 10: [2]}
 
 FLOPS = 2 * K * S * S2 + 2 * 2 * S * N * S2
 
@@ -90,8 +79,6 @@ def tile_list_region_patch_pool_kernel(
             queue.dma_start(v_tab_sc[32 * q : 32 * q + 8, :], tab_scales[:, 4 * q : 4 * q + 4, :].bitcast(I32))
         nc.sync.dma_start(pw_sb[:, :, 0:PACK], pw.rearrange("(b p t) -> p b t", p=P, t=PACK))
         nc.sync.dma_start(v_tab[0][:], words_of(tab_words, 0))
-        if XEARLY:
-            load_x(0)
         nc.sync.dma_start(v_tab[1][:], words_of(tab_words, 1))
         def load_g4():
             for q in range(4):
@@ -101,12 +88,16 @@ def tile_list_region_patch_pool_kernel(
                 )
             nc.sync.dma_start(g4_w[:].bitcast(I32), g4_words.rearrange("a p c -> p a c").bitcast(I32))
 
-        for b in range(XEARLY, NB):
-            if b == G4POS:
-                load_g4()
-            load_x(b)
-        if G4POS == NB:
-            load_g4()
+        load_x(0)
+        load_x(1)
+        load_g4()
+        load_x(2)
+
+        pw_half = []
+        for k in range(NB * JC):
+            half = keep.tile([P, PACK], F32, name=f"pw_half{k}", tag=f"after_step{k}", align_bytes=64)
+            nc.scalar.mul(half[:], pw_sb[:, k // JC, 0:PACK], 0.5)
+            pw_half.append(half)
 
         v2_w = [keep.tile([P, S2], U32, name=f"v2_w{a}", align_bytes=64) for a in range(KP)]
         v2_sc = keep.tile([P, S2], U8, name="v2_sc", align_bytes=64)
@@ -126,21 +117,29 @@ def tile_list_region_patch_pool_kernel(
                 v_w[a][b][:].rearrange("p (t m) -> p m t", t=PACK), v_tab[a][:].bitcast(U32).indirect(entries(b))
             )
 
-        for b in range(NB):
-            nc.vector.tensor_copy(v_sc_list[:, b * PASS : (b + 1) * PASS], v_tab_sc[:].bitcast(U8).indirect(entries(b)))
-        nc.vector.tensor_copy(
-            v_sc[:].rearrange("p (b t m) -> p t b m", b=NB, t=PACK),
-            v_sc_list[:].rearrange("p (b m t) -> p t b m", b=NB, t=PACK),
-        )
+        parts = ((0, NB - 1), (NB - 1, NB))
+        for b0, b1 in parts:
+            nc.vector.tensor_copy(
+                v_sc_list[:, b0 * PASS : b1 * PASS],
+                v_tab_sc[:].bitcast(U8).indirect(idx[:, b0 * LIST_COLS : b1 * LIST_COLS]),
+            )
+        for b0, b1 in parts:
+            nc.vector.tensor_copy(
+                v_sc[:, b0 * PASS : b1 * PASS].rearrange("p (b t m) -> p t b m", t=PACK, m=P),
+                v_sc_list[:, b0 * PASS : b1 * PASS].rearrange("p (b m t) -> p t b m", t=PACK, m=P),
+            )
         for b in range(NB):
             gather_words(0, b)
 
         x_bf = [keep.tile([P, N * PACK], BF16, name=f"x_bf{b}", align_bytes=64) for b in range(NB)]
         x_w = [keep.tile([P, N], U32, name=f"x_w{b}", align_bytes=64) for b in range(NB)]
-        x_sc = [keep.tile([P, N], U8, name=f"x_sc{b}", align_bytes=64) for b in range(NB)]
         h_bf = [keep.tile([P, S2 * PACK], BF16, name=f"h_bf{b}", align_bytes=64) for b in range(NB)]
         h_w = [keep.tile([P, S2], U32, name=f"h_w{b}", align_bytes=64) for b in range(NB)]
-        h_sc = [keep.tile([P, S2], U8, name=f"h_sc{b}", align_bytes=64) for b in range(NB)]
+        x_sc, h_sc = {}, {}
+
+        def scale_tile(name, width, after_step):
+            tag = name if after_step is None else f"after_step{after_step}"
+            return keep.tile([P, width], U8, name=name, tag=tag, align_bytes=64)
 
         def cast_x(copy, b, c0, c1):
             if b == 0:
@@ -163,10 +162,17 @@ def tile_list_region_patch_pool_kernel(
                     ALU.add,
                 )
 
-        def quantize_x(b):
-            nc.vector.quantize_mx(out=x_w[b][:].bitcast(E4M3), scales=x_sc[b][:], in_=x_bf[b][:])
+        def quantize_x(b, n0, n1, after_step):
+            scales = scale_tile(f"x_sc{b}_{n0}", (n1 - n0) * P, after_step)
+            for n in range(n0, n1):
+                x_sc[b, n] = scales[:, (n - n0) * P : (n - n0 + 1) * P]
+            nc.vector.quantize_mx(
+                out=x_w[b][:, n0 * P : n1 * P].bitcast(E4M3), scales=scales[:], in_=x_bf[b][:, n0 * PASS : n1 * PASS]
+            )
 
-        def quantize_h(b, c0, c1):
+        def quantize_h(b, c0, c1, after_step):
+            if c0 == 0:
+                h_sc[b] = scale_tile(f"h_sc{b}", S2, after_step)
             nc.vector.quantize_mx(
                 out=h_w[b][:, c0 * P : c1 * P].bitcast(E4M3),
                 scales=h_sc[b][:, c0 * P : c1 * P],
@@ -192,7 +198,7 @@ def tile_list_region_patch_pool_kernel(
             else:
                 weighted = ring.tile([P, PACK, U_STEP], F32, name="weighted")
             for t in range(PACK):
-                nc.scalar.activation(weighted[:, t, 0:P], bank[:, t, :], ACT.Copy, scale=pw_sb[:, b, t : t + 1])
+                nc.scalar.activation(weighted[:, t, 0:P], bank[:, t, :], ACT.Copy, scale=pw_half[b * JC + c][:, t : t + 1])
             nc.vector.scalar_tensor_tensor(
                 out=h_bf[b][:, c * PASS : (c + 1) * PASS].rearrange("p (j t) -> p j t", t=PACK),
                 in0=bank[:].rearrange("p t j -> p j t"),
@@ -217,7 +223,7 @@ def tile_list_region_patch_pool_kernel(
             nc.tensor.matmul_mx(
                 out=acc[:],
                 lhsT=x_w[b][:, n * P : (n + 1) * P].bitcast(E4M3),
-                lhsT_scale=x_sc[b][:, n * P : (n + 1) * P],
+                lhsT_scale=x_sc[b, n],
                 rhs=h_w[b][:].bitcast(E4M3),
                 rhs_scale=h_sc[b][:],
                 start=(b == 0),
@@ -233,39 +239,57 @@ def tile_list_region_patch_pool_kernel(
             (gate_pass if kind == "g" else value_pass)(accs[n], n, b)
 
         cast_x_gpsimd(1)
-        for xb, xc in SCASTS.get(-1, []):
-            cast_x(nc.scalar.copy, xb, xc, xc + 1)
-        for xb in QX.get(-1, []):
-            quantize_x(xb)
+        cast_x(nc.scalar.copy, 0, 0, 1)
+        cast_x(nc.scalar.copy, 0, 1, 2)
         for b in range(NB):
             gather_words(1, b)
         for k in range(NB * JC):
             b, c = divmod(k, JC)
             scores(b, c)
-            for qb, c0, c1 in QH.get(k, []):
-                quantize_h(qb, c0, c1)
-            for xb, xc in SCASTS.get(k, []):
-                cast_x(nc.scalar.copy, xb, xc, xc + 1)
-            for xb, xc0, xc1 in VCASTS.get(k, []):
-                cast_x(nc.vector.tensor_copy, xb, xc0, xc1)
-            for xb in QX.get(k, []):
-                quantize_x(xb)
-            for kind, n, pb in POOL.get(k, []):
-                pool(kind, n, pb)
+            if k == 4:
+                quantize_h(0, 0, JC, k)
+            if k in (4, 5):
+                cast_x(nc.scalar.copy, 0, k - 2, k - 1)
+            if k == 5:
+                quantize_x(0, 0, NT, None)
+                for kind in "gy":
+                    for n in (0, 1):
+                        pool(kind, n, 0)
+            if k == 7:
+                quantize_x(1, 0, NT, k)
+                quantize_h(1, 0, JC, None)
+            if k in (7, 8):
+                cast_x(nc.scalar.copy, 2, k - 7, k - 6)
+            if k == 9:
+                for n in (0, 1):
+                    pool("g", n, 1)
+                    pool("y", n, 1)
+            if k == 10:
+                quantize_h(2, 0, 2, k)
+                quantize_h(2, 2, 3, None)
+            if k == 11:
+                quantize_x(2, 0, 2, k)
+                quantize_h(2, 3, 4, None)
+                cast_x(nc.scalar.copy, 2, 2, 3)
+                cast_x(nc.scalar.copy, 2, 3, 4)
+                quantize_x(2, 2, 4, None)
+                for n in (2, 3):
+                    for kind in "gy":
+                        for pb in (0, 1):
+                            pool(kind, n, pb)
 
         for n in range(NT):
-            gate_pass(g_acc[n], n, NB - 1)
-            if n == NT - 1:
-                for b in range(NB - 1):
-                    pool("y", n, b)
-            value_pass(y_acc[n], n, NB - 1)
+            pool("g", n, NB - 1)
+            pool("y", n, NB - 1)
             gate = keep.tile([P, S2], F32, name=f"gate{n}")
             res = keep.tile([P, S2], F32, name=f"res{n}")
             pieces = 2 if n in (0, NT - 1) else 1
             for h in range(pieces):
                 cols = slice(h * S2 // pieces, (h + 1) * S2 // pieces)
-                nc.scalar.activation(gate[:, cols], g_acc[n][:, cols], ACT.Sigmoid)
-                nc.vector.tensor_tensor(res[:, cols], y_acc[n][:, cols], gate[:, cols], ALU.mult)
+                nc.scalar.activation(gate[:, cols], g_acc[n][:, cols], ACT.Tanh)
+                nc.vector.scalar_tensor_tensor(
+                    out=res[:, cols], in0=gate[:, cols], scalar=1.0, in1=y_acc[n][:, cols], op0=ALU.add, op1=ALU.mult
+                )
                 if n == NT - 1:
                     nc.sync.dma_start(out[n * P : (n + 1) * P, cols], res[:, cols])
             if n < NT - 1:

@@ -27,7 +27,7 @@ U_STEP = P + 1
 RING = 4
 SBANK = [0, 1, 2, 3, 4, 5, 0, 1, 2, 3, 0, 1]
 ABANK = {"g": [6, 7, 2, 0], "y": [4, 5, 3, 1]}
-GW = 64
+GW = 256
 
 FLOPS = 2 * K * S * S2 + 2 * 2 * S * N * S2
 
@@ -43,7 +43,7 @@ def tile_list_region_patch_pool_kernel(
 
         idx = keep.tile([P, S // 16], U16, name="idx")
         idx2 = keep.tile([P, S2 // 16], U16, name="idx2")
-        v_tab = [keep.tile([P, T], I32, name=f"v_tab{a}", align_bytes=64) for a in range(KP)]
+        v_tab = [keep.tile([P, T], I32, name=f"v_tab{a}", tag=f"v_tab{a}", align_bytes=64) for a in range(KP)]
         v2_tab = [keep.tile([P, T2], I32, name=f"v2_tab{a}", align_bytes=64) for a in range(KP)]
         v_tab_sc = keep.tile([P, T // 4], I32, name="v_tab_sc", align_bytes=64)
         v2_tab_sc = keep.tile([P, T2 // 4], I32, name="v2_tab_sc", align_bytes=64)
@@ -131,7 +131,10 @@ def tile_list_region_patch_pool_kernel(
         for b in range(NB):
             gather_words(0, b)
 
-        x_bf = [keep.tile([P, N * PACK], BF16, name=f"x_bf{b}", align_bytes=64) for b in range(NB)]
+        x_bf = [
+            keep.tile([P, N * PACK], BF16, name=f"x_bf{b}", tag="v_tab1" if b == 1 else f"x_bf{b}", align_bytes=64)
+            for b in range(NB)
+        ]
         x_w = [keep.tile([P, N], U32, name=f"x_w{b}", align_bytes=64) for b in range(NB)]
         h_bf = [keep.tile([P, S2 * PACK], BF16, name=f"h_bf{b}", align_bytes=64) for b in range(NB)]
         h_w = [keep.tile([P, S2], U32, name=f"h_w{b}", align_bytes=64) for b in range(NB)]
@@ -208,25 +211,25 @@ def tile_list_region_patch_pool_kernel(
                 op1=ALU.mult,
             )
 
-        def gate_pass(acc, n, b):
+        def gate_pass(acc, n, b, first):
             nc.tensor.matmul_mx(
                 out=acc[:],
                 lhsT=g4_w[:, b, 2 * n * P : 2 * (n + 1) * P].bitcast(E2M1),
                 lhsT_scale=g4_sc[:, b, :].bitcast(U8)[:, n * P : (n + 1) * P],
                 rhs=h_w[b][:].bitcast(E4M3),
                 rhs_scale=h_sc[b][:],
-                start=(b == 0),
+                start=first,
                 stop=(b == NB - 1),
             )
 
-        def value_pass(acc, n, b):
+        def value_pass(acc, n, b, first):
             nc.tensor.matmul_mx(
                 out=acc[:],
                 lhsT=x_w[b][:, n * P : (n + 1) * P].bitcast(E4M3),
                 lhsT_scale=x_sc[b, n],
                 rhs=h_w[b][:].bitcast(E4M3),
                 rhs_scale=h_sc[b][:],
-                start=(b == 0),
+                start=first,
                 stop=(b == NB - 1),
             )
 
@@ -234,36 +237,28 @@ def tile_list_region_patch_pool_kernel(
 
         def pool(kind, n, b):
             accs = g_acc if kind == "g" else y_acc
-            if b == 0:
+            first = n not in accs
+            if first:
                 accs[n] = psum.tile([P, S2], F32, name=f"{kind}_acc{n}", tag=f"bank{ABANK[kind][n]}")
-            (gate_pass if kind == "g" else value_pass)(accs[n], n, b)
+            (gate_pass if kind == "g" else value_pass)(accs[n], n, b, first)
 
-        cast_x_gpsimd(1)
         cast_x(nc.scalar.copy, 0, 0, 1)
         cast_x(nc.scalar.copy, 0, 1, 2)
         for b in range(NB):
             gather_words(1, b)
+        cast_x_gpsimd(1)
         for k in range(NB * JC):
             b, c = divmod(k, JC)
             scores(b, c)
-            if k == 4:
-                quantize_h(0, 0, JC, k)
-            if k in (4, 5):
-                cast_x(nc.scalar.copy, 0, k - 2, k - 1)
-            if k == 5:
-                quantize_x(0, 0, NT, None)
-                for kind in "gy":
-                    for n in (0, 1):
-                        pool(kind, n, 0)
-            if k == 7:
+            if k == 6:
                 quantize_x(1, 0, NT, k)
-                quantize_h(1, 0, JC, None)
             if k in (7, 8):
-                cast_x(nc.scalar.copy, 2, k - 7, k - 6)
-            if k == 9:
-                for n in (0, 1):
-                    pool("g", n, 1)
-                    pool("y", n, 1)
+                quantize_h(k - 7, 0, JC, k)
+                cast_x(nc.scalar.copy, 0, k - 5, k - 4)
+            if k == 8:
+                quantize_x(0, 0, NT, None)
+            if k in (9, 10):
+                cast_x(nc.scalar.copy, 2, k - 9, k - 8)
             if k == 10:
                 quantize_h(2, 0, 2, k)
                 quantize_h(2, 2, 3, None)
@@ -273,6 +268,10 @@ def tile_list_region_patch_pool_kernel(
                 cast_x(nc.scalar.copy, 2, 2, 3)
                 cast_x(nc.scalar.copy, 2, 3, 4)
                 quantize_x(2, 2, 4, None)
+                for kind, order in (("g", (0, 1)), ("y", (1, 0))):
+                    for pb in order:
+                        for n in (0, 1):
+                            pool(kind, n, pb)
                 for n in (2, 3):
                     for kind in "gy":
                         for pb in (0, 1):

@@ -28,6 +28,7 @@ RING = 4
 SBANK = [0, 1, 2, 3, 4, 5, 0, 1, 2, 3, 0, 1]
 ABANK = {"g": [6, 7, 2, 0], "y": [4, 5, 3, 1]}
 GW = 256
+SPLIT = T // 4
 
 FLOPS = 2 * K * S * S2 + 2 * 2 * S * N * S2
 
@@ -51,7 +52,8 @@ def tile_list_region_patch_pool_kernel(
         g4_sc = keep.tile([P, NB, N // 4], I32, name="g4_sc", align_bytes=64)
         pw_sb = keep.tile([P, NB, 8], F32, name="pw_sb")
         x_raw = [keep.tile([P, PACK, N], F32, name=f"x_raw{b}", align_bytes=64) for b in range(1, NB)]
-        x_half = [keep.tile([P, PACK, N // 2], F32, name=f"x_half{h}", tag=f"x_half{h}", align_bytes=64) for h in range(2)]
+        x_first = keep.tile([P, PACK, P], F32, name="x_first", tag="x_first", align_bytes=64)
+        x_rest = keep.tile([P, PACK, N - P], F32, name="x_rest", align_bytes=64)
 
         nc.vector.memset(v2_tab_sc[:], 0)
         nc.gpsimd.memset(v_tab_sc[:], 0)
@@ -60,63 +62,25 @@ def tile_list_region_patch_pool_kernel(
         def words_of(table, a):
             return table[a].rearrange("p t i -> p (t i)").bitcast(I32)
 
-        def load_x(b):
-            rows = x[b * PASS : (b + 1) * PASS, :].rearrange("(p t) n -> p t n", t=PACK)
-            if b == 0:
-                for h in range(2):
-                    nc.sync.dma_start(x_half[h][:], rows[:, :, h * N // 2 : (h + 1) * N // 2])
-            else:
-                nc.sync.dma_start(x_raw[b - 1][:], rows)
+        def x_rows(b):
+            return x[b * PASS : (b + 1) * PASS, :].rearrange("(p t) n -> p t n", t=PACK)
 
-        nc.sync.dma_start(idx2[:], offs2)
         nc.sync.dma_start(v2_tab[0][:], words_of(tab2_words, 0))
+        nc.sync.dma_start(idx2[:], offs2)
         nc.sync.dma_start(idx[:], offs)
+        nc.sync.dma_start(v_tab_sc[0:P:4, :], tab_scales.rearrange("a r c -> r a c").bitcast(I32))
         nc.sync.dma_start(v2_tab[1][:], words_of(tab2_words, 1))
         for q in range(4):
             nc.sync.dma_start(v2_tab_sc[32 * q + 8 : 32 * q + 16, :], tab2_scales[:, 4 * q : 4 * q + 4, :].bitcast(I32))
-        for q in range(4):
-            queue = nc.gpsimd if q % 2 else nc.sync
-            queue.dma_start(v_tab_sc[32 * q : 32 * q + 8, :], tab_scales[:, 4 * q : 4 * q + 4, :].bitcast(I32))
         nc.sync.dma_start(pw_sb[:, :, 0:PACK], pw.rearrange("(b p t) -> p b t", p=P, t=PACK))
         nc.sync.dma_start(v_tab[0][:], words_of(tab_words, 0))
-        nc.sync.dma_start(v_tab[1][:], words_of(tab_words, 1))
-        def load_g4():
-            for q in range(4):
-                nc.sync.dma_start(
-                    g4_sc[32 * q : 32 * q + 4, :, :],
-                    g4_scales[:, 4 * q : 4 * q + 4, :].rearrange("a r c -> r a c").bitcast(I32),
-                )
-            nc.sync.dma_start(g4_w[:].bitcast(I32), g4_words.rearrange("a p c -> p a c").bitcast(I32))
-
-        load_x(0)
-        load_x(1)
-        load_g4()
-        load_x(2)
-
-        pw_half = []
-        for k in range(NB * JC):
-            half = keep.tile([P, PACK], F32, name=f"pw_half{k}", tag=f"after_step{k}", align_bytes=64)
-            nc.scalar.mul(half[:], pw_sb[:, k // JC, 0:PACK], 0.5)
-            pw_half.append(half)
+        nc.sync.dma_start(v_tab[1][:, 0:SPLIT], words_of(tab_words, 1)[:, 0:SPLIT])
 
         v2_w = [keep.tile([P, S2], U32, name=f"v2_w{a}", align_bytes=64) for a in range(KP)]
         v2_sc = keep.tile([P, S2], U8, name="v2_sc", align_bytes=64)
-        for a in range(KP):
-            nc.vector.tensor_copy(v2_w[a][:], v2_tab[a][:].bitcast(U32).indirect(idx2[:]))
-        nc.vector.tensor_copy(v2_sc[:], v2_tab_sc[:].bitcast(U8).indirect(idx2[:]))
-
-        v_w = [[keep.tile([P, PASS], U32, name=f"v_w{a}_{b}", align_bytes=64) for b in range(NB)] for a in range(KP)]
         v_sc_list = keep.tile([P, S], U8, name="v_sc_list", align_bytes=64)
         v_sc = keep.tile([P, S], U8, name="v_sc", align_bytes=64)
-
-        def entries(b):
-            return idx[:, b * LIST_COLS : (b + 1) * LIST_COLS]
-
-        def gather_words(a, b):
-            nc.vector.tensor_copy(
-                v_w[a][b][:].rearrange("p (t m) -> p m t", t=PACK), v_tab[a][:].bitcast(U32).indirect(entries(b))
-            )
-
+        nc.vector.tensor_copy(v2_w[0][:], v2_tab[0][:].bitcast(U32).indirect(idx2[:]))
         parts = ((0, NB - 1), (NB - 1, NB))
         for b0, b1 in parts:
             nc.vector.tensor_copy(
@@ -128,8 +92,47 @@ def tile_list_region_patch_pool_kernel(
                 v_sc[:, b0 * PASS : b1 * PASS].rearrange("p (b t m) -> p t b m", t=PACK, m=P),
                 v_sc_list[:, b0 * PASS : b1 * PASS].rearrange("p (b m t) -> p t b m", t=PACK, m=P),
             )
-        for b in range(NB):
-            gather_words(0, b)
+        for a in range(KP):
+            for r in range(1, 4):
+                nc.sync.dma_start(v_sc[4 * a + r : P : 32, :].bitcast(I32), v_sc[4 * a + 8 * r : P : 32, :].bitcast(I32))
+        nc.sync.dma_start(v_tab[1][:, SPLIT:T], words_of(tab_words, 1)[:, SPLIT:T])
+
+        def load_g4():
+            for q in range(4):
+                nc.sync.dma_start(
+                    g4_sc[32 * q : 32 * q + 4, :, :],
+                    g4_scales[:, 4 * q : 4 * q + 4, :].rearrange("a r c -> r a c").bitcast(I32),
+                )
+            nc.sync.dma_start(g4_w[:].bitcast(I32), g4_words.rearrange("a p c -> p a c").bitcast(I32))
+
+        nc.sync.dma_start(x_first[:], x_rows(0)[:, :, 0:P])
+        nc.sync.dma_start(x_raw[0][:], x_rows(1))
+        nc.sync.dma_start(x_rest[:], x_rows(0)[:, :, P:N])
+        load_g4()
+        nc.sync.dma_start(x_raw[1][:], x_rows(2))
+
+        pw_half = []
+        for k in range(NB * JC):
+            half = keep.tile([P, PACK], F32, name=f"pw_half{k}", tag=f"after_step{k}", align_bytes=64)
+            nc.scalar.mul(half[:], pw_sb[:, k // JC, 0:PACK], 0.5)
+            pw_half.append([half[:, t : t + 1] for t in range(PACK)])
+        last = keep.tile([P, 1], F32, name="pw_half8x", tag="after_step8x", align_bytes=64)
+        nc.scalar.mul(last[:], pw_sb[:, 2, PACK - 1 : PACK], 0.5)
+        pw_half[8][PACK - 1] = last[:]
+
+        nc.vector.tensor_copy(v2_w[1][:], v2_tab[1][:].bitcast(U32).indirect(idx2[:]))
+        nc.vector.tensor_copy(v2_sc[:], v2_tab_sc[:].bitcast(U8).indirect(idx2[:]))
+
+        v_w = [keep.tile([P, S], U32, name=f"v_w{a}", align_bytes=64) for a in range(KP)]
+
+        def gather_words(a):
+            for b0, b1 in ((0, 1), (1, NB)):
+                nc.vector.tensor_copy(
+                    v_w[a][:, b0 * PASS : b1 * PASS].rearrange("p (b t m) -> p b m t", t=PACK, m=P),
+                    v_tab[a][:].bitcast(U32).indirect(idx[:, b0 * LIST_COLS : b1 * LIST_COLS]),
+                )
+
+        gather_words(0)
 
         x_bf = [
             keep.tile([P, N * PACK], BF16, name=f"x_bf{b}", tag="v_tab1" if b == 1 else f"x_bf{b}", align_bytes=64)
@@ -146,7 +149,7 @@ def tile_list_region_patch_pool_kernel(
 
         def cast_x(copy, b, c0, c1):
             if b == 0:
-                src = x_half[c0 // 2][:, :, (c0 % 2) * P : (c0 % 2 + c1 - c0) * P]
+                src = x_first[:] if c0 == 0 else x_rest[:, :, (c0 - 1) * P : (c1 - 1) * P]
             else:
                 src = x_raw[b - 1][:, :, c0 * P : c1 * P]
             copy(
@@ -154,16 +157,15 @@ def tile_list_region_patch_pool_kernel(
                 src.rearrange("p t (c i) -> p c t i", i=4),
             )
 
-        def cast_x_gpsimd(b):
-            for j0 in range(0, N, GW):
-                nc.gpsimd.tensor_scalar(
-                    x_bf[b][:, j0 * PACK : (j0 + GW) * PACK].rearrange("p (j t) -> p j t", t=PACK),
-                    x_raw[b - 1][:, :, j0 : j0 + GW].rearrange("p t j -> p j t"),
-                    1.0,
-                    0.0,
-                    ALU.mult,
-                    ALU.add,
-                )
+        def cast_x_gpsimd(b, src, j0):
+            nc.gpsimd.tensor_scalar(
+                x_bf[b][:, j0 * PACK : (j0 + src.shape[2]) * PACK].rearrange("p (j t) -> p j t", t=PACK),
+                src.rearrange("p t j -> p j t"),
+                1.0,
+                0.0,
+                ALU.mult,
+                ALU.add,
+            )
 
         def quantize_x(b, n0, n1, after_step):
             scales = scale_tile(f"x_sc{b}_{n0}", (n1 - n0) * P, after_step)
@@ -189,7 +191,7 @@ def tile_list_region_patch_pool_kernel(
                 for t in range(PACK):
                     nc.tensor.matmul_mx(
                         out=bank[:, t, :],
-                        lhsT=v_w[a][b][:, t * P : (t + 1) * P].bitcast(E4M3),
+                        lhsT=v_w[a][:, b * PASS + t * P : b * PASS + (t + 1) * P].bitcast(E4M3),
                         lhsT_scale=v_sc[4 * a :, b * PASS + t * P : b * PASS + (t + 1) * P],
                         rhs=v2_w[a][:, cols].bitcast(E4M3),
                         rhs_scale=v2_sc[8 + 4 * a :, cols],
@@ -197,11 +199,11 @@ def tile_list_region_patch_pool_kernel(
                         stop=(a == KP - 1 and t == PACK - 1),
                     )
             if b == 0 and c == 0:
-                weighted = keep.tile([P, PACK, U_STEP], F32, name="weighted", tag="x_half0", align_bytes=64)
+                weighted = keep.tile([P, PACK, U_STEP], F32, name="weighted", tag="x_first", align_bytes=64)
             else:
                 weighted = ring.tile([P, PACK, U_STEP], F32, name="weighted")
             for t in range(PACK):
-                nc.scalar.activation(weighted[:, t, 0:P], bank[:, t, :], ACT.Copy, scale=pw_half[b * JC + c][:, t : t + 1])
+                nc.scalar.activation(weighted[:, t, 0:P], bank[:, t, :], ACT.Copy, scale=pw_half[b * JC + c][t])
             nc.vector.scalar_tensor_tensor(
                 out=h_bf[b][:, c * PASS : (c + 1) * PASS].rearrange("p (j t) -> p j t", t=PACK),
                 in0=bank[:].rearrange("p t j -> p j t"),
@@ -243,20 +245,20 @@ def tile_list_region_patch_pool_kernel(
             (gate_pass if kind == "g" else value_pass)(accs[n], n, b, first)
 
         cast_x(nc.scalar.copy, 0, 0, 1)
-        cast_x(nc.scalar.copy, 0, 1, 2)
-        for b in range(NB):
-            gather_words(1, b)
-        cast_x_gpsimd(1)
+        gather_words(1)
+        cast_x_gpsimd(1, x_raw[0][:, :, 0:GW], 0)
+        cast_x_gpsimd(0, x_rest[:, :, 0:P], P)
+        cast_x_gpsimd(1, x_raw[0][:, :, GW:N], GW)
         for k in range(NB * JC):
             b, c = divmod(k, JC)
             scores(b, c)
-            if k == 6:
-                quantize_x(1, 0, NT, k)
             if k in (7, 8):
                 quantize_h(k - 7, 0, JC, k)
                 cast_x(nc.scalar.copy, 0, k - 5, k - 4)
             if k == 8:
-                quantize_x(0, 0, NT, None)
+                quantize_x(1, 0, NT, "8x")
+            if k == 9:
+                quantize_x(0, 0, NT, k)
             if k in (9, 10):
                 cast_x(nc.scalar.copy, 2, k - 9, k - 8)
             if k == 10:

@@ -116,9 +116,6 @@ def tile_list_region_patch_pool_kernel(
             half = keep.tile([P, PACK], F32, name=f"pw_half{k}", tag=f"after_step{k}", align_bytes=64)
             nc.scalar.mul(half[:], pw_sb[:, k // JC, 0:PACK], 0.5)
             pw_half.append([half[:, t : t + 1] for t in range(PACK)])
-        last = keep.tile([P, 1], F32, name="pw_half8x", tag="after_step8x", align_bytes=64)
-        nc.scalar.mul(last[:], pw_sb[:, 2, PACK - 1 : PACK], 0.5)
-        pw_half[8][PACK - 1] = last[:]
 
         nc.vector.tensor_copy(v2_w[1][:], v2_tab[1][:].bitcast(U32).indirect(idx2[:]))
         nc.vector.tensor_copy(v2_sc[:], v2_tab_sc[:].bitcast(U8).indirect(idx2[:]))
@@ -252,21 +249,22 @@ def tile_list_region_patch_pool_kernel(
         for k in range(NB * JC):
             b, c = divmod(k, JC)
             scores(b, c)
-            if k in (7, 8):
-                quantize_h(k - 7, 0, JC, k)
-                cast_x(nc.scalar.copy, 0, k - 5, k - 4)
-            if k == 8:
-                quantize_x(1, 0, NT, "8x")
-            if k == 9:
-                quantize_x(0, 0, NT, k)
+            if k == 6:
+                quantize_h(0, 0, JC, k)
+            if k == 7:
+                quantize_x(1, 0, NT, k)
+                quantize_h(1, 0, JC, None)
+                cast_x(nc.scalar.copy, 0, 2, 3)
+                cast_x(nc.scalar.copy, 0, 3, 4)
+                quantize_x(0, 0, NT, None)
             if k in (9, 10):
                 cast_x(nc.scalar.copy, 2, k - 9, k - 8)
             if k == 10:
                 quantize_h(2, 0, 2, k)
                 quantize_h(2, 2, 3, None)
             if k == 11:
-                quantize_x(2, 0, 2, k)
                 quantize_h(2, 3, 4, None)
+                quantize_x(2, 0, 2, k)
                 cast_x(nc.scalar.copy, 2, 2, 3)
                 cast_x(nc.scalar.copy, 2, 3, 4)
                 quantize_x(2, 2, 4, None)
@@ -274,22 +272,37 @@ def tile_list_region_patch_pool_kernel(
                     for pb in order:
                         for n in (0, 1):
                             pool(kind, n, pb)
-                for n in (2, 3):
-                    for kind in "gy":
-                        for pb in (0, 1):
-                            pool(kind, n, pb)
+                for kind, n in (("g", 2), ("y", 2), ("g", 3)):
+                    for pb in (0, 1):
+                        pool(kind, n, pb)
 
         for n in range(NT):
             pool("g", n, NB - 1)
-            pool("y", n, NB - 1)
+            if n < NT - 1:
+                pool("y", n, NB - 1)
             gate = keep.tile([P, S2], F32, name=f"gate{n}")
             res = keep.tile([P, S2], F32, name=f"res{n}")
-            pieces = 2 if n in (0, NT - 1) else 1
+            pieces = 2
             for h in range(pieces):
                 cols = slice(h * S2 // pieces, (h + 1) * S2 // pieces)
+                if n == NT - 1:
+                    y_part = psum.tile([P, S2 // 2], F32, name=f"y_last{h}", tag=f"bank{(ABANK['y'][n], ABANK['g'][0])[h]}")
+                    for pb in range(NB):
+                        nc.tensor.matmul_mx(
+                            out=y_part[:],
+                            lhsT=x_w[pb][:, n * P : (n + 1) * P].bitcast(E4M3),
+                            lhsT_scale=x_sc[pb, n],
+                            rhs=h_w[pb][:, cols].bitcast(E4M3),
+                            rhs_scale=h_sc[pb][:, cols],
+                            start=(pb == 0),
+                            stop=(pb == NB - 1),
+                        )
+                    y_cols = y_part[:]
+                else:
+                    y_cols = y_acc[n][:, cols]
                 nc.scalar.activation(gate[:, cols], g_acc[n][:, cols], ACT.Tanh)
                 nc.vector.scalar_tensor_tensor(
-                    out=res[:, cols], in0=gate[:, cols], scalar=1.0, in1=y_acc[n][:, cols], op0=ALU.add, op1=ALU.mult
+                    out=res[:, cols], in0=gate[:, cols], scalar=1.0, in1=y_cols, op0=ALU.add, op1=ALU.mult
                 )
                 if n == NT - 1:
                     nc.sync.dma_start(out[n * P : (n + 1) * P, cols], res[:, cols])

@@ -28,6 +28,7 @@ RING = 4
 SBANK = [0, 1, 2, 3, 4, 5, 0, 1, 2, 3, 0, 1]
 ABANK = {"g": [6, 7, 2, 0], "y": [4, 5, 3, 1]}
 GW = 256
+SPARED = 8
 SPLIT = T // 4
 
 FLOPS = 2 * K * S * S2 + 2 * 2 * S * N * S2
@@ -111,11 +112,15 @@ def tile_list_region_patch_pool_kernel(
         load_g4()
         nc.sync.dma_start(x_raw[1][:], x_rows(2))
 
-        pw_half = []
+        pw_half, pw_tile = [], []
         for k in range(NB * JC):
             half = keep.tile([P, PACK], F32, name=f"pw_half{k}", tag=f"after_step{k}", align_bytes=64)
             nc.scalar.mul(half[:], pw_sb[:, k // JC, 0:PACK], 0.5)
             pw_half.append([half[:, t : t + 1] for t in range(PACK)])
+            pw_tile.append(half)
+        last = keep.tile([P, 1], F32, name="pw_half7x", tag="after_step7x", align_bytes=64)
+        nc.scalar.mul(last[:], pw_sb[:, 1, PACK - 1 : PACK], 0.5)
+        pw_half[7][PACK - 1] = last[:]
 
         nc.vector.tensor_copy(v2_w[1][:], v2_tab[1][:].bitcast(U32).indirect(idx2[:]))
         nc.vector.tensor_copy(v2_sc[:], v2_tab_sc[:].bitcast(U8).indirect(idx2[:]))
@@ -139,6 +144,7 @@ def tile_list_region_patch_pool_kernel(
         h_bf = [keep.tile([P, S2 * PACK], BF16, name=f"h_bf{b}", align_bytes=64) for b in range(NB)]
         h_w = [keep.tile([P, S2], U32, name=f"h_w{b}", align_bytes=64) for b in range(NB)]
         x_sc, h_sc = {}, {}
+        h_spared = []
 
         def scale_tile(name, width, after_step):
             tag = name if after_step is None else f"after_step{after_step}"
@@ -178,7 +184,7 @@ def tile_list_region_patch_pool_kernel(
             nc.vector.quantize_mx(
                 out=h_w[b][:, c0 * P : c1 * P].bitcast(E4M3),
                 scales=h_sc[b][:, c0 * P : c1 * P],
-                in_=h_bf[b][:, c0 * PASS : c1 * PASS],
+                in_=h_spared[0][:] if b * JC + c0 == SPARED else h_bf[b][:, c0 * PASS : c1 * PASS],
             )
 
         def scores(b, c):
@@ -195,6 +201,21 @@ def tile_list_region_patch_pool_kernel(
                         start=(a == 0 and t == 0),
                         stop=(a == KP - 1 and t == PACK - 1),
                     )
+            if b * JC + c == SPARED:
+                kept = keep.tile([P, PASS], F32, name="kept", align_bytes=64)
+                squared = keep.tile([P, PASS], F32, name="squared", align_bytes=64)
+                nc.scalar.activation(
+                    kept[:].rearrange("p (j t) -> p j t", t=PACK), bank[:].rearrange("p t j -> p j t"), ACT.Relu
+                )
+                nc.scalar.activation(squared[:], kept[:], ACT.Square)
+                h_spared.append(keep.tile([P, PASS], BF16, name="h_spared", tag="x_bf0", align_bytes=64))
+                nc.gpsimd.tensor_tensor(
+                    h_spared[0][:].rearrange("p (j t) -> p j t", t=PACK),
+                    squared[:].rearrange("p (j t) -> p j t", t=PACK),
+                    pw_tile[SPARED][:].unsqueeze(1).to_broadcast([P, P, PACK]),
+                    ALU.mult,
+                )
+                return
             if b == 0 and c == 0:
                 weighted = keep.tile([P, PACK, U_STEP], F32, name="weighted", tag="x_first", align_bytes=64)
             else:
@@ -244,24 +265,22 @@ def tile_list_region_patch_pool_kernel(
         cast_x(nc.scalar.copy, 0, 0, 1)
         gather_words(1)
         cast_x_gpsimd(1, x_raw[0][:, :, 0:GW], 0)
-        cast_x_gpsimd(0, x_rest[:, :, 0:P], P)
+        cast_x_gpsimd(0, x_rest[:, :, 0 : 2 * P], P)
         cast_x_gpsimd(1, x_raw[0][:, :, GW:N], GW)
         for k in range(NB * JC):
             b, c = divmod(k, JC)
             scores(b, c)
-            if k == 6:
-                quantize_h(0, 0, JC, k)
             if k == 7:
-                quantize_x(1, 0, NT, k)
+                quantize_h(0, 0, JC, k)
                 quantize_h(1, 0, JC, None)
-                cast_x(nc.scalar.copy, 0, 2, 3)
+                quantize_x(1, 0, NT, "7x")
                 cast_x(nc.scalar.copy, 0, 3, 4)
                 quantize_x(0, 0, NT, None)
             if k in (9, 10):
                 cast_x(nc.scalar.copy, 2, k - 9, k - 8)
             if k == 10:
-                quantize_h(2, 0, 2, k)
-                quantize_h(2, 2, 3, None)
+                quantize_h(2, 0, 1, k)
+                quantize_h(2, 1, 3, None)
             if k == 11:
                 quantize_h(2, 3, 4, None)
                 quantize_x(2, 0, 2, k)

@@ -29,7 +29,7 @@ SBANK = [0, 1, 2, 3, 4, 5, 0, 1, 2, 3, 0, 1]
 ABANK = {"g": [6, 7, 2, 0], "y": [4, 5, 3, 1]}
 GW = 256
 SPARED = 8
-SPLIT = T // 4
+SPLIT = T // 2
 
 FLOPS = 2 * K * S * S2 + 2 * 2 * S * N * S2
 
@@ -179,7 +179,7 @@ def tile_list_region_patch_pool_kernel(
             )
 
         def quantize_h(b, c0, c1, after_step):
-            if c0 == 0:
+            if b not in h_sc:
                 h_sc[b] = scale_tile(f"h_sc{b}", S2, after_step)
             nc.vector.quantize_mx(
                 out=h_w[b][:, c0 * P : c1 * P].bitcast(E4M3),
@@ -276,14 +276,14 @@ def tile_list_region_patch_pool_kernel(
                 quantize_x(1, 0, NT, "7x")
                 cast_x(nc.scalar.copy, 0, 3, 4)
                 quantize_x(0, 0, NT, None)
-            if k in (9, 10):
-                cast_x(nc.scalar.copy, 2, k - 9, k - 8)
-            if k == 10:
-                quantize_h(2, 0, 1, k)
-                quantize_h(2, 1, 3, None)
+            if k == 9:
+                cast_x(nc.scalar.copy, 2, 0, 1)
             if k == 11:
+                quantize_h(2, 1, 3, k)
+                quantize_h(2, 0, 1, None)
                 quantize_h(2, 3, 4, None)
-                quantize_x(2, 0, 2, k)
+                cast_x(nc.scalar.copy, 2, 1, 2)
+                quantize_x(2, 0, 2, None)
                 cast_x(nc.scalar.copy, 2, 2, 3)
                 cast_x(nc.scalar.copy, 2, 3, 4)
                 quantize_x(2, 2, 4, None)
@@ -301,11 +301,16 @@ def tile_list_region_patch_pool_kernel(
                 pool("y", n, NB - 1)
             gate = keep.tile([P, S2], F32, name=f"gate{n}")
             res = keep.tile([P, S2], F32, name=f"res{n}")
-            pieces = 2
-            for h in range(pieces):
-                cols = slice(h * S2 // pieces, (h + 1) * S2 // pieces)
+            edges = (0, 2 * P, 3 * P, S2) if n == NT - 1 else (0, 2 * P, S2)
+            for h in range(len(edges) - 1):
+                cols = slice(edges[h], edges[h + 1])
                 if n == NT - 1:
-                    y_part = psum.tile([P, S2 // 2], F32, name=f"y_last{h}", tag=f"bank{(ABANK['y'][n], ABANK['g'][0])[h]}")
+                    y_part = psum.tile(
+                        [P, edges[h + 1] - edges[h]],
+                        F32,
+                        name=f"y_last{h}",
+                        tag=f"bank{(ABANK['y'][n], ABANK['g'][0], ABANK['g'][1])[h]}",
+                    )
                     for pb in range(NB):
                         nc.tensor.matmul_mx(
                             out=y_part[:],
@@ -323,7 +328,7 @@ def tile_list_region_patch_pool_kernel(
                 nc.vector.scalar_tensor_tensor(
                     out=res[:, cols], in0=gate[:, cols], scalar=1.0, in1=y_cols, op0=ALU.add, op1=ALU.mult
                 )
-                if n == NT - 1:
+                if n in (0, NT - 1):
                     nc.sync.dma_start(out[n * P : (n + 1) * P, cols], res[:, cols])
-            if n < NT - 1:
+            if 0 < n < NT - 1:
                 nc.sync.dma_start(out[n * P : (n + 1) * P, :], res[:])

@@ -29,6 +29,7 @@ SBANK = [0, 1, 2, 3, 4, 5, 0, 1, 2, 3, 0, 1]
 ABANK = {"g": [6, 7, 2, 0], "y": [4, 5, 3, 1]}
 GW = 256
 SPARED = 8
+EARLY_SPARED = 3
 SPLIT = T // 2
 
 FLOPS = 2 * K * S * S2 + 2 * 2 * S * N * S2
@@ -201,18 +202,22 @@ def tile_list_region_patch_pool_kernel(
                         start=(a == 0 and t == 0),
                         stop=(a == KP - 1 and t == PACK - 1),
                     )
-            if b * JC + c == SPARED:
-                kept = keep.tile([P, PASS], F32, name="kept", align_bytes=64)
-                squared = keep.tile([P, PASS], F32, name="squared", align_bytes=64)
+            if b * JC + c in (EARLY_SPARED, SPARED):
+                kept = keep.tile([P, PASS], F32, name=f"kept{b}", align_bytes=64)
+                squared = keep.tile([P, PASS], F32, name=f"squared{b}", align_bytes=64)
                 nc.scalar.activation(
                     kept[:].rearrange("p (j t) -> p j t", t=PACK), bank[:].rearrange("p t j -> p j t"), ACT.Relu
                 )
                 nc.scalar.activation(squared[:], kept[:], ACT.Square)
-                h_spared.append(keep.tile([P, PASS], BF16, name="h_spared", tag="x_bf0", align_bytes=64))
+                if b * JC + c == SPARED:
+                    h_spared.append(keep.tile([P, PASS], BF16, name="h_spared", tag="x_bf0", align_bytes=64))
+                    h_out = h_spared[0][:]
+                else:
+                    h_out = h_bf[b][:, c * PASS : (c + 1) * PASS]
                 nc.gpsimd.tensor_tensor(
-                    h_spared[0][:].rearrange("p (j t) -> p j t", t=PACK),
+                    h_out.rearrange("p (j t) -> p j t", t=PACK),
                     squared[:].rearrange("p (j t) -> p j t", t=PACK),
-                    pw_tile[SPARED][:].unsqueeze(1).to_broadcast([P, P, PACK]),
+                    pw_tile[b * JC + c][:].unsqueeze(1).to_broadcast([P, P, PACK]),
                     ALU.mult,
                 )
                 return

@@ -22,15 +22,17 @@ NB = S // PASS
 JC = S2 // P
 NT = N // P
 LIST_COLS = PASS // 16
-U_STEP = P + 1
+SLOT_PITCH = P + 1
 
-RING = 4
-SBANK = [0, 1, 2, 3, 4, 5, 0, 1, 2, 3, 0, 1]
-ABANK = {"g": [6, 7, 2, 0], "y": [4, 5, 3, 1]}
-GW = 256
-SPARED = 8
-EARLY_SPARED = 3
-SPLIT = T // 2
+WEIGHTED_BUFS = 4
+SCORE_BANK = [0, 1, 2, 3, 4, 5, 0, 1, 2, 3, 0, 1]
+SUM_BANK = {"g": [6, 7, 2, 0], "y": [4, 5, 3, 1]}
+EARLY_STEPS = 2
+GPSIMD_STEP = 8
+CLEAR_SPLIT = 640
+V2_AT = 4 * T + 6144 + 4096
+G4_AT = 0
+GP_STEPS = (8,)
 
 FLOPS = 2 * K * S * S2 + 2 * 2 * S * N * S2
 
@@ -41,48 +43,69 @@ def tile_list_region_patch_pool_kernel(
     nc = tc.nc
     with ExitStack() as ctx:
         keep = ctx.enter_context(tc.tile_pool(name="keep", bufs=1))
-        ring = ctx.enter_context(tc.tile_pool(name="ring", bufs=RING))
+        ring = ctx.enter_context(tc.tile_pool(name="ring", bufs=WEIGHTED_BUFS))
         psum = ctx.enter_context(tc.psum_pool(name="psum", bufs=1))
+
+        shared = ctx.enter_context(tc.tile_pool(name="shared", bufs=1))
+
+        def tile(name, shape, dtype, on=None):
+            if isinstance(on, int):
+                return shared.tile(shape, dtype, name=name, offset=on, align_bytes=64)
+            return keep.tile(shape, dtype, name=name, tag=on or name, align_bytes=64)
 
         idx = keep.tile([P, S // 16], U16, name="idx")
         idx2 = keep.tile([P, S2 // 16], U16, name="idx2")
-        v_tab = [keep.tile([P, T], I32, name=f"v_tab{a}", tag=f"v_tab{a}", align_bytes=64) for a in range(KP)]
-        v2_tab = [keep.tile([P, T2], I32, name=f"v2_tab{a}", align_bytes=64) for a in range(KP)]
-        v_tab_sc = keep.tile([P, T // 4], I32, name="v_tab_sc", align_bytes=64)
-        v2_tab_sc = keep.tile([P, T2 // 4], I32, name="v2_tab_sc", align_bytes=64)
-        g4_w = keep.tile([P, NB, 2 * N], U8, name="g4_w", align_bytes=64)
-        g4_sc = keep.tile([P, NB, N // 4], I32, name="g4_sc", align_bytes=64)
-        pw_sb = keep.tile([P, NB, 8], F32, name="pw_sb")
-        x_raw = [keep.tile([P, PACK, N], F32, name=f"x_raw{b}", align_bytes=64) for b in range(1, NB)]
-        x_first = keep.tile([P, PACK, P], F32, name="x_first", tag="x_first", align_bytes=64)
-        x_rest = keep.tile([P, PACK, N - P], F32, name="x_rest", align_bytes=64)
+        v_tab = [tile(f"v_tab{a}", [P, T], I32, on=0 if a == 0 else None) for a in range(KP)]
+        v2_tab = [tile(f"v2_tab{a}", [P, T2], I32, on=V2_AT if a == 1 else None) for a in range(KP)]
+        v_tab_sc = tile("v_tab_sc", [P, T // 4], I32)
+        v2_tab_sc = tile("v2_tab_sc", [P, T2 // 4], I32)
 
-        nc.vector.memset(v2_tab_sc[:], 0)
-        nc.gpsimd.memset(v_tab_sc[:], 0)
-        nc.vector.memset(g4_sc[:], 0)
+        nc.gpsimd.memset(v2_tab_sc[:], 0)
+        nc.vector.memset(v_tab_sc[:, 0:CLEAR_SPLIT], 0)
+        nc.gpsimd.memset(v_tab_sc[:, CLEAR_SPLIT:], 0)
 
         def words_of(table, a):
             return table[a].rearrange("p t i -> p (t i)").bitcast(I32)
 
-        def x_rows(b):
-            return x[b * PASS : (b + 1) * PASS, :].rearrange("(p t) n -> p t n", t=PACK)
+        def spread_rows(scales):
+            return scales.rearrange("a r c -> r a c").bitcast(I32)
 
-        nc.sync.dma_start(v2_tab[0][:], words_of(tab2_words, 0))
+        x_raw = {}
+
+        def load_x(b, q0, q1, on=None):
+            raw = tile(f"x_raw{b}_{q0}", [P, PACK, (q1 - q0) * P], F32, on)
+            rows = x[b * PASS : (b + 1) * PASS, :].rearrange("(p t) n -> p t n", t=PACK)
+            nc.sync.dma_start(raw[:], rows[:, :, q0 * P : q1 * P])
+            for q in range(q0, q1):
+                x_raw[b, q] = (raw, q - q0)
+
         nc.sync.dma_start(idx2[:], offs2)
         nc.sync.dma_start(idx[:], offs)
-        nc.sync.dma_start(v_tab_sc[0:P:4, :], tab_scales.rearrange("a r c -> r a c").bitcast(I32))
+        nc.sync.dma_start(v2_tab_sc[0:P:4, :], spread_rows(tab2_scales))
+        nc.sync.dma_start(v2_tab[0][:], words_of(tab2_words, 0))
+        nc.sync.dma_start(v_tab_sc[0:P:4, :], spread_rows(tab_scales))
         nc.sync.dma_start(v2_tab[1][:], words_of(tab2_words, 1))
-        for q in range(4):
-            nc.sync.dma_start(v2_tab_sc[32 * q + 8 : 32 * q + 16, :], tab2_scales[:, 4 * q : 4 * q + 4, :].bitcast(I32))
-        nc.sync.dma_start(pw_sb[:, :, 0:PACK], pw.rearrange("(b p t) -> p b t", p=P, t=PACK))
         nc.sync.dma_start(v_tab[0][:], words_of(tab_words, 0))
-        nc.sync.dma_start(v_tab[1][:, 0:SPLIT], words_of(tab_words, 1)[:, 0:SPLIT])
 
-        v2_w = [keep.tile([P, S2], U32, name=f"v2_w{a}", align_bytes=64) for a in range(KP)]
-        v2_sc = keep.tile([P, S2], U8, name="v2_sc", align_bytes=64)
-        v_sc_list = keep.tile([P, S], U8, name="v_sc_list", align_bytes=64)
-        v_sc = keep.tile([P, S], U8, name="v_sc", align_bytes=64)
-        nc.vector.tensor_copy(v2_w[0][:], v2_tab[0][:].bitcast(U32).indirect(idx2[:]))
+        nc.sync.dma_start(v_tab[1][:], words_of(tab_words, 1))
+
+        v2_w = [tile(f"v2_w{a}", [P, S2], U32) for a in range(KP)]
+        v_w = [tile(f"v_w{a}", [P, S], U32) for a in range(KP)]
+        v2_sc_list = tile("v2_sc_list", [P, S2], U8)
+        v_sc_list = tile("v_sc_list", [P, S], U8)
+        tab_sc = tile("tab_sc", [P, S + S2], U8)
+
+        def gather_small(a):
+            nc.vector.tensor_copy(v2_w[a][:], v2_tab[a][:].bitcast(U32).indirect(idx2[:]))
+
+        def gather_words(a, b0, b1):
+            nc.vector.tensor_copy(
+                v_w[a][:, b0 * PASS : b1 * PASS].rearrange("p (b t m) -> p b m t", t=PACK, m=P),
+                v_tab[a][:].bitcast(U32).indirect(idx[:, b0 * LIST_COLS : b1 * LIST_COLS]),
+            )
+
+        nc.vector.tensor_copy(v2_sc_list[:], v2_tab_sc[:].bitcast(U8).indirect(idx2[:]))
+        gather_small(0)
         parts = ((0, NB - 1), (NB - 1, NB))
         for b0, b1 in parts:
             nc.vector.tensor_copy(
@@ -91,142 +114,130 @@ def tile_list_region_patch_pool_kernel(
             )
         for b0, b1 in parts:
             nc.vector.tensor_copy(
-                v_sc[:, b0 * PASS : b1 * PASS].rearrange("p (b t m) -> p t b m", t=PACK, m=P),
+                tab_sc[:, b0 * PASS : b1 * PASS].rearrange("p (b t m) -> p t b m", t=PACK, m=P),
                 v_sc_list[:, b0 * PASS : b1 * PASS].rearrange("p (b m t) -> p t b m", t=PACK, m=P),
             )
+        nc.vector.tensor_copy(tab_sc[:, S:].bitcast(I32), v2_sc_list[:].bitcast(I32))
         for a in range(KP):
             for r in range(1, 4):
-                nc.sync.dma_start(v_sc[4 * a + r : P : 32, :].bitcast(I32), v_sc[4 * a + 8 * r : P : 32, :].bitcast(I32))
-        nc.sync.dma_start(v_tab[1][:, SPLIT:T], words_of(tab_words, 1)[:, SPLIT:T])
-
-        def load_g4():
-            for q in range(4):
                 nc.sync.dma_start(
-                    g4_sc[32 * q : 32 * q + 4, :, :],
-                    g4_scales[:, 4 * q : 4 * q + 4, :].rearrange("a r c -> r a c").bitcast(I32),
+                    tab_sc[4 * a + r : P : 32, :].bitcast(I32), tab_sc[4 * a + 8 * r : P : 32, :].bitcast(I32)
                 )
-            nc.sync.dma_start(g4_w[:].bitcast(I32), g4_words.rearrange("a p c -> p a c").bitcast(I32))
-
-        nc.sync.dma_start(x_first[:], x_rows(0)[:, :, 0:P])
-        nc.sync.dma_start(x_raw[0][:], x_rows(1))
-        nc.sync.dma_start(x_rest[:], x_rows(0)[:, :, P:N])
-        load_g4()
-        nc.sync.dma_start(x_raw[1][:], x_rows(2))
+        gather_small(1)
+        pw_sb = tile("pw_sb", [P, NB, 8], F32, on=V2_AT + 64)
+        nc.sync.dma_start(pw_sb[:, :, 0:PACK], pw.rearrange("(b p t) -> p b t", p=P, t=PACK))
+        load_x(0, 0, 1, on=V2_AT + 192)
+        load_x(1, 0, 4, on=V2_AT + 192 + 2112)
+        load_x(0, 1, 4, on=V2_AT + 64 - 6144)
+        gather_words(0, 0, 1)
+        gather_words(0, 1, NB)
 
         pw_half, pw_tile = [], []
         for k in range(NB * JC):
-            half = keep.tile([P, PACK], F32, name=f"pw_half{k}", tag=f"after_step{k}", align_bytes=64)
+            half = tile(f"after_step{k}", [P, PACK], F32)
             nc.scalar.mul(half[:], pw_sb[:, k // JC, 0:PACK], 0.5)
             pw_half.append([half[:, t : t + 1] for t in range(PACK)])
             pw_tile.append(half)
-        last = keep.tile([P, 1], F32, name="pw_half7x", tag="after_step7x", align_bytes=64)
+        last = tile("after_step7x", [P, 1], F32)
         nc.scalar.mul(last[:], pw_sb[:, 1, PACK - 1 : PACK], 0.5)
         pw_half[7][PACK - 1] = last[:]
 
-        nc.vector.tensor_copy(v2_w[1][:], v2_tab[1][:].bitcast(U32).indirect(idx2[:]))
-        nc.vector.tensor_copy(v2_sc[:], v2_tab_sc[:].bitcast(U8).indirect(idx2[:]))
+        g4_sb = tile("g4_sb", [P, NB * 3 * N], U8, on=G4_AT)
+        g4_w = g4_sb[:, 0 : NB * 2 * N].rearrange("p (b c) -> p b c", b=NB)
+        g4_sc = g4_sb[:, NB * 2 * N :].rearrange("p (b c) -> p b c", b=NB)
+        for q in range(4):
+            nc.sync.dma_start(
+                g4_sc[32 * q : 32 * q + 4, :, :].bitcast(I32), spread_rows(g4_scales[:, 4 * q : 4 * q + 4, :])
+            )
+        nc.sync.dma_start(g4_w.bitcast(I32), g4_words.rearrange("a p c -> p a c").bitcast(I32))
 
-        v_w = [keep.tile([P, S], U32, name=f"v_w{a}", align_bytes=64) for a in range(KP)]
+        x_bf = [tile(f"x_bf{b}", [P, N * PACK], BF16, on="v_tab1" if b == 1 else None) for b in range(NB)]
+        x_w = [tile(f"x_w{b}", [P, N], U32) for b in range(NB)]
+        h_bf = [tile(f"h_bf{b}", [P, S2 * PACK], BF16) for b in range(NB)]
+        h_w = [tile(f"h_w{b}", [P, S2], U32) for b in range(NB)]
+        x_sc, h_sc, h_gpsimd = {}, {}, []
 
-        def gather_words(a):
-            for b0, b1 in ((0, 1), (1, NB)):
-                nc.vector.tensor_copy(
-                    v_w[a][:, b0 * PASS : b1 * PASS].rearrange("p (b t m) -> p b m t", t=PACK, m=P),
-                    v_tab[a][:].bitcast(U32).indirect(idx[:, b0 * LIST_COLS : b1 * LIST_COLS]),
-                )
-
-        gather_words(0)
-
-        x_bf = [
-            keep.tile([P, N * PACK], BF16, name=f"x_bf{b}", tag="v_tab1" if b == 1 else f"x_bf{b}", align_bytes=64)
-            for b in range(NB)
-        ]
-        x_w = [keep.tile([P, N], U32, name=f"x_w{b}", align_bytes=64) for b in range(NB)]
-        h_bf = [keep.tile([P, S2 * PACK], BF16, name=f"h_bf{b}", align_bytes=64) for b in range(NB)]
-        h_w = [keep.tile([P, S2], U32, name=f"h_w{b}", align_bytes=64) for b in range(NB)]
-        x_sc, h_sc = {}, {}
-        h_spared = []
-
-        def scale_tile(name, width, after_step):
-            tag = name if after_step is None else f"after_step{after_step}"
-            return keep.tile([P, width], U8, name=name, tag=tag, align_bytes=64)
-
-        def cast_x(copy, b, c0, c1):
-            if b == 0:
-                src = x_first[:] if c0 == 0 else x_rest[:, :, (c0 - 1) * P : (c1 - 1) * P]
-            else:
-                src = x_raw[b - 1][:, :, c0 * P : c1 * P]
-            copy(
-                x_bf[b][:, c0 * PASS : c1 * PASS].rearrange("p (c i t) -> p c t i", i=4, t=PACK),
-                src.rearrange("p t (c i) -> p c t i", i=4),
+        def cast_x(b, q):
+            raw, at = x_raw[b, q]
+            nc.scalar.copy(
+                x_bf[b][:, q * PASS : (q + 1) * PASS].rearrange("p (c i t) -> p c t i", i=4, t=PACK),
+                raw[:, :, at * P : (at + 1) * P].rearrange("p t (c i) -> p c t i", i=4),
             )
 
-        def cast_x_gpsimd(b, src, j0):
+        def cast_x_gpsimd(b, q0, q1):
+            raw, at = x_raw[b, q0]
             nc.gpsimd.tensor_scalar(
-                x_bf[b][:, j0 * PACK : (j0 + src.shape[2]) * PACK].rearrange("p (j t) -> p j t", t=PACK),
-                src.rearrange("p t j -> p j t"),
+                x_bf[b][:, q0 * PASS : q1 * PASS].rearrange("p (j t) -> p j t", t=PACK),
+                raw[:, :, at * P : (at + q1 - q0) * P].rearrange("p t j -> p j t"),
                 1.0,
                 0.0,
                 ALU.mult,
                 ALU.add,
             )
 
-        def quantize_x(b, n0, n1, after_step):
-            scales = scale_tile(f"x_sc{b}_{n0}", (n1 - n0) * P, after_step)
+        def quantize_x(b, n0, n1, on=None):
+            scales = tile(f"x_sc{b}_{n0}", [P, (n1 - n0) * P], U8, on)
             for n in range(n0, n1):
                 x_sc[b, n] = scales[:, (n - n0) * P : (n - n0 + 1) * P]
             nc.vector.quantize_mx(
                 out=x_w[b][:, n0 * P : n1 * P].bitcast(E4M3), scales=scales[:], in_=x_bf[b][:, n0 * PASS : n1 * PASS]
             )
 
-        def quantize_h(b, c0, c1, after_step):
+        def quantize_h(b, c0, c1, on=None):
             if b not in h_sc:
-                h_sc[b] = scale_tile(f"h_sc{b}", S2, after_step)
+                h_sc[b] = tile(f"h_sc{b}", [P, S2], U8, on)
             nc.vector.quantize_mx(
                 out=h_w[b][:, c0 * P : c1 * P].bitcast(E4M3),
                 scales=h_sc[b][:, c0 * P : c1 * P],
-                in_=h_spared[0][:] if b * JC + c0 == SPARED else h_bf[b][:, c0 * PASS : c1 * PASS],
+                in_=h_gpsimd[0][:] if b * JC + c0 == GPSIMD_STEP else h_bf[b][:, c0 * PASS : c1 * PASS],
             )
 
-        def scores(b, c):
-            bank = psum.tile([P, PACK, P], F32, name="bank", tag=f"bank{SBANK[b * JC + c]}")
-            cols = slice(c * P, (c + 1) * P)
-            for a in range(KP):
-                for t in range(PACK):
-                    nc.tensor.matmul_mx(
-                        out=bank[:, t, :],
-                        lhsT=v_w[a][:, b * PASS + t * P : b * PASS + (t + 1) * P].bitcast(E4M3),
-                        lhsT_scale=v_sc[4 * a :, b * PASS + t * P : b * PASS + (t + 1) * P],
-                        rhs=v2_w[a][:, cols].bitcast(E4M3),
-                        rhs_scale=v2_sc[8 + 4 * a :, cols],
-                        start=(a == 0 and t == 0),
-                        stop=(a == KP - 1 and t == PACK - 1),
-                    )
-            if b * JC + c in (EARLY_SPARED, SPARED):
-                kept = keep.tile([P, PASS], F32, name=f"kept{b}", align_bytes=64)
-                squared = keep.tile([P, PASS], F32, name=f"squared{b}", align_bytes=64)
+        banks = {}
+
+        def score_pass(k, a):
+            b, c = divmod(k, JC)
+            if a == 0:
+                banks[k] = psum.tile([P, PACK, P], F32, name="bank", tag=f"bank{SCORE_BANK[k]}")
+            for t in range(PACK):
+                slot = slice(b * PASS + t * P, b * PASS + (t + 1) * P)
+                nc.tensor.matmul_mx(
+                    out=banks[k][:, t, :],
+                    lhsT=v_w[a][:, slot].bitcast(E4M3),
+                    lhsT_scale=tab_sc[4 * a :, slot],
+                    rhs=v2_w[a][:, c * P : (c + 1) * P].bitcast(E4M3),
+                    rhs_scale=tab_sc[4 * a :, S + c * P : S + (c + 1) * P],
+                    start=(a == 0 and t == 0),
+                    stop=(a == KP - 1 and t == PACK - 1),
+                )
+
+        def make_h(k, on=None):
+            b, c = divmod(k, JC)
+            bank = banks[k]
+            if k in GP_STEPS:
+                kept = tile(f"kept{k}", [P, PASS], F32, on)
+                squared = tile(f"squared{k}", [P, PASS], F32)
                 nc.scalar.activation(
                     kept[:].rearrange("p (j t) -> p j t", t=PACK), bank[:].rearrange("p t j -> p j t"), ACT.Relu
                 )
                 nc.scalar.activation(squared[:], kept[:], ACT.Square)
-                if b * JC + c == SPARED:
-                    h_spared.append(keep.tile([P, PASS], BF16, name="h_spared", tag="x_bf0", align_bytes=64))
-                    h_out = h_spared[0][:]
+                if k == GPSIMD_STEP:
+                    h_gpsimd.append(tile("h_gpsimd", [P, PASS], BF16, on="x_bf0"))
+                    h_out = h_gpsimd[0][:]
                 else:
                     h_out = h_bf[b][:, c * PASS : (c + 1) * PASS]
                 nc.gpsimd.tensor_tensor(
                     h_out.rearrange("p (j t) -> p j t", t=PACK),
                     squared[:].rearrange("p (j t) -> p j t", t=PACK),
-                    pw_tile[b * JC + c][:].unsqueeze(1).to_broadcast([P, P, PACK]),
+                    pw_tile[k][:].unsqueeze(1).to_broadcast([P, P, PACK]),
                     ALU.mult,
                 )
                 return
-            if b == 0 and c == 0:
-                weighted = keep.tile([P, PACK, U_STEP], F32, name="weighted", tag="x_first", align_bytes=64)
+            if on is not None:
+                weighted = tile(f"weighted{k}", [P, PACK, SLOT_PITCH], F32, on)
             else:
-                weighted = ring.tile([P, PACK, U_STEP], F32, name="weighted")
+                weighted = ring.tile([P, PACK, SLOT_PITCH], F32, name="weighted")
             for t in range(PACK):
-                nc.scalar.activation(weighted[:, t, 0:P], bank[:, t, :], ACT.Copy, scale=pw_half[b * JC + c][t])
+                nc.scalar.activation(weighted[:, t, 0:P], bank[:, t, :], ACT.Copy, scale=pw_half[k][t])
             nc.vector.scalar_tensor_tensor(
                 out=h_bf[b][:, c * PASS : (c + 1) * PASS].rearrange("p (j t) -> p j t", t=PACK),
                 in0=bank[:].rearrange("p t j -> p j t"),
@@ -236,62 +247,62 @@ def tile_list_region_patch_pool_kernel(
                 op1=ALU.mult,
             )
 
-        def gate_pass(acc, n, b, first):
+        sums = {}
+
+        def pool_pass(acc, kind, n, b, cols):
+            if kind == "g":
+                lhsT = g4_w[:, b, 2 * n * P : 2 * (n + 1) * P].bitcast(E2M1)
+                lhsT_scale = g4_sc[:, b, n * P : (n + 1) * P]
+            else:
+                lhsT = x_w[b][:, n * P : (n + 1) * P].bitcast(E4M3)
+                lhsT_scale = x_sc[b, n]
+            first = acc not in sums
+            if first:
+                sums[acc] = psum.tile([P, cols.stop - cols.start], F32, name="sum", tag=f"bank{acc[1]}")
             nc.tensor.matmul_mx(
-                out=acc[:],
-                lhsT=g4_w[:, b, 2 * n * P : 2 * (n + 1) * P].bitcast(E2M1),
-                lhsT_scale=g4_sc[:, b, :].bitcast(U8)[:, n * P : (n + 1) * P],
-                rhs=h_w[b][:].bitcast(E4M3),
-                rhs_scale=h_sc[b][:],
+                out=sums[acc][:],
+                lhsT=lhsT,
+                lhsT_scale=lhsT_scale,
+                rhs=h_w[b][:, cols].bitcast(E4M3),
+                rhs_scale=h_sc[b][:, cols],
                 start=first,
                 stop=(b == NB - 1),
             )
-
-        def value_pass(acc, n, b, first):
-            nc.tensor.matmul_mx(
-                out=acc[:],
-                lhsT=x_w[b][:, n * P : (n + 1) * P].bitcast(E4M3),
-                lhsT_scale=x_sc[b, n],
-                rhs=h_w[b][:].bitcast(E4M3),
-                rhs_scale=h_sc[b][:],
-                start=first,
-                stop=(b == NB - 1),
-            )
-
-        g_acc, y_acc = {}, {}
 
         def pool(kind, n, b):
-            accs = g_acc if kind == "g" else y_acc
-            first = n not in accs
-            if first:
-                accs[n] = psum.tile([P, S2], F32, name=f"{kind}_acc{n}", tag=f"bank{ABANK[kind][n]}")
-            (gate_pass if kind == "g" else value_pass)(accs[n], n, b, first)
+            pool_pass(((kind, n), SUM_BANK[kind][n]), kind, n, b, slice(0, S2))
 
-        cast_x(nc.scalar.copy, 0, 0, 1)
-        gather_words(1)
-        cast_x_gpsimd(1, x_raw[0][:, :, 0:GW], 0)
-        cast_x_gpsimd(0, x_rest[:, :, 0 : 2 * P], P)
-        cast_x_gpsimd(1, x_raw[0][:, :, GW:N], GW)
+        load_x(2, 0, NT, on=G4_AT + 4608)
+        cast_x(0, 0)
+        for k in range(EARLY_STEPS):
+            score_pass(k, 0)
+        gather_words(1, 0, 1)
+        gather_words(1, 1, NB)
+        cast_x_gpsimd(1, 0, 2)
+        cast_x_gpsimd(0, 1, 3)
+        cast_x_gpsimd(1, 2, 4)
         for k in range(NB * JC):
-            b, c = divmod(k, JC)
-            scores(b, c)
+            if k >= EARLY_STEPS:
+                score_pass(k, 0)
+            score_pass(k, 1)
+            make_h(k, on=V2_AT + 192 - 64 + 64 if k == 0 else None)
             if k == 7:
-                quantize_h(0, 0, JC, k)
-                quantize_h(1, 0, JC, None)
-                quantize_x(1, 0, NT, "7x")
-                cast_x(nc.scalar.copy, 0, 3, 4)
-                quantize_x(0, 0, NT, None)
+                quantize_h(0, 0, JC, on="after_step7")
+                quantize_h(1, 0, JC)
+                quantize_x(1, 0, NT, on="after_step7x")
+                cast_x(0, 3)
+                quantize_x(0, 0, NT)
             if k == 9:
-                cast_x(nc.scalar.copy, 2, 0, 1)
+                cast_x(2, 0)
             if k == 11:
-                quantize_h(2, 1, 3, k)
-                quantize_h(2, 0, 1, None)
-                quantize_h(2, 3, 4, None)
-                cast_x(nc.scalar.copy, 2, 1, 2)
-                quantize_x(2, 0, 2, None)
-                cast_x(nc.scalar.copy, 2, 2, 3)
-                cast_x(nc.scalar.copy, 2, 3, 4)
-                quantize_x(2, 2, 4, None)
+                quantize_h(2, 1, 3, on="after_step11")
+                quantize_h(2, 0, 1)
+                quantize_h(2, 3, 4)
+                cast_x(2, 1)
+                quantize_x(2, 0, 2)
+                cast_x(2, 2)
+                cast_x(2, 3)
+                quantize_x(2, 2, 4)
                 for kind, order in (("g", (0, 1)), ("y", (1, 0))):
                     for pb in order:
                         for n in (0, 1):
@@ -304,32 +315,20 @@ def tile_list_region_patch_pool_kernel(
             pool("g", n, NB - 1)
             if n < NT - 1:
                 pool("y", n, NB - 1)
+            g_sum = sums[("g", n), SUM_BANK["g"][n]]
             gate = keep.tile([P, S2], F32, name=f"gate{n}")
             res = keep.tile([P, S2], F32, name=f"res{n}")
             edges = (0, 2 * P, 3 * P, S2) if n == NT - 1 else (0, 2 * P, S2)
             for h in range(len(edges) - 1):
                 cols = slice(edges[h], edges[h + 1])
                 if n == NT - 1:
-                    y_part = psum.tile(
-                        [P, edges[h + 1] - edges[h]],
-                        F32,
-                        name=f"y_last{h}",
-                        tag=f"bank{(ABANK['y'][n], ABANK['g'][0], ABANK['g'][1])[h]}",
-                    )
-                    for pb in range(NB):
-                        nc.tensor.matmul_mx(
-                            out=y_part[:],
-                            lhsT=x_w[pb][:, n * P : (n + 1) * P].bitcast(E4M3),
-                            lhsT_scale=x_sc[pb, n],
-                            rhs=h_w[pb][:, cols].bitcast(E4M3),
-                            rhs_scale=h_sc[pb][:, cols],
-                            start=(pb == 0),
-                            stop=(pb == NB - 1),
-                        )
-                    y_cols = y_part[:]
+                    acc = (("y", n, h), (SUM_BANK["y"][n], SUM_BANK["g"][0], SUM_BANK["g"][1])[h])
+                    for b in range(NB):
+                        pool_pass(acc, "y", n, b, cols)
+                    y_cols = sums[acc][:]
                 else:
-                    y_cols = y_acc[n][:, cols]
-                nc.scalar.activation(gate[:, cols], g_acc[n][:, cols], ACT.Tanh)
+                    y_cols = sums[("y", n), SUM_BANK["y"][n]][:, cols]
+                nc.scalar.activation(gate[:, cols], g_sum[:, cols], ACT.Tanh)
                 nc.vector.scalar_tensor_tensor(
                     out=res[:, cols], in0=gate[:, cols], scalar=1.0, in1=y_cols, op0=ALU.add, op1=ALU.mult
                 )

@@ -273,6 +273,17 @@ def tile_list_region_patch_pool_kernel(
             pool_pass(((kind, n), SUM_BANK[kind][n]), kind, n, b, slice(0, S2))
 
         load_x(2, 0, NT, on=G4_AT + 4608)
+        warm = psum.tile([P, PASS], F32, name="warm", tag="bank7")
+        for w in range(4):
+            nc.tensor.matmul_mx(
+                out=warm[:],
+                lhsT=v2_w[0][:, w * P : (w + 1) * P].bitcast(E4M3),
+                lhsT_scale=v2_sc_list[:, w * P : (w + 1) * P],
+                rhs=v_w[0][:, 0:PASS].bitcast(E4M3),
+                rhs_scale=v_sc_list[:, 0:PASS],
+                start=True,
+                stop=True,
+            )
         cast_x(0, 0)
         for k in range(EARLY_STEPS):
             score_pass(k, 0)

@@ -32,6 +32,7 @@ GPSIMD_STEP = 8
 CLEAR_SPLIT = 640
 V2_AT = 4 * T + 6144 + 4096
 G4_AT = 0
+HOLD_AT = V2_AT + 16384
 GP_STEPS = (8,)
 
 FLOPS = 2 * K * S * S2 + 2 * 2 * S * N * S2
@@ -124,23 +125,19 @@ def tile_list_region_patch_pool_kernel(
                     tab_sc[4 * a + r : P : 32, :].bitcast(I32), tab_sc[4 * a + 8 * r : P : 32, :].bitcast(I32)
                 )
         gather_small(1)
+        load_x(0, 0, 1, on=V2_AT + 192)
         pw_sb = tile("pw_sb", [P, NB, 8], F32, on=V2_AT + 64)
         nc.sync.dma_start(pw_sb[:, :, 0:PACK], pw.rearrange("(b p t) -> p b t", p=P, t=PACK))
-        load_x(0, 0, 1, on=V2_AT + 192)
         load_x(1, 0, 4, on=V2_AT + 192 + 2112)
         load_x(0, 1, 4, on=V2_AT + 64 - 6144)
         gather_words(0, 0, 1)
         gather_words(0, 1, NB)
 
-        pw_half, pw_tile = [], []
-        for k in range(NB * JC):
-            half = tile(f"after_step{k}", [P, PACK], F32)
-            nc.scalar.mul(half[:], pw_sb[:, k // JC, 0:PACK], 0.5)
-            pw_half.append([half[:, t : t + 1] for t in range(PACK)])
-            pw_tile.append(half)
-        last = tile("after_step7x", [P, 1], F32)
-        nc.scalar.mul(last[:], pw_sb[:, 1, PACK - 1 : PACK], 0.5)
-        pw_half[7][PACK - 1] = last[:]
+        pw_of = {k: pw_sb[:, k // JC, 0:PACK] for k in range(NB * JC)}
+
+        def own_weights(k, width):
+            pw_of[k] = tile(f"after_step{k}", [P, width // 4], F32, on=HOLD_AT + (k // 11) * 2 * S2)[:, 0:PACK]
+            nc.scalar.copy(pw_of[k], pw_sb[:, k // JC, 0:PACK])
 
         g4_sb = tile("g4_sb", [P, NB * 3 * N], U8, on=G4_AT)
         g4_w = g4_sb[:, 0 : NB * 2 * N].rearrange("p (b c) -> p b c", b=NB)
@@ -159,9 +156,10 @@ def tile_list_region_patch_pool_kernel(
 
         def cast_x(b, q):
             raw, at = x_raw[b, q]
-            nc.scalar.copy(
+            nc.scalar.mul(
                 x_bf[b][:, q * PASS : (q + 1) * PASS].rearrange("p (c i t) -> p c t i", i=4, t=PACK),
                 raw[:, :, at * P : (at + 1) * P].rearrange("p t (c i) -> p c t i", i=4),
+                0.5,
             )
 
         def cast_x_gpsimd(b, q0, q1):
@@ -169,7 +167,7 @@ def tile_list_region_patch_pool_kernel(
             nc.gpsimd.tensor_scalar(
                 x_bf[b][:, q0 * PASS : q1 * PASS].rearrange("p (j t) -> p j t", t=PACK),
                 raw[:, :, at * P : (at + q1 - q0) * P].rearrange("p t j -> p j t"),
-                1.0,
+                0.5,
                 0.0,
                 ALU.mult,
                 ALU.add,
@@ -228,7 +226,7 @@ def tile_list_region_patch_pool_kernel(
                 nc.gpsimd.tensor_tensor(
                     h_out.rearrange("p (j t) -> p j t", t=PACK),
                     squared[:].rearrange("p (j t) -> p j t", t=PACK),
-                    pw_tile[k][:].unsqueeze(1).to_broadcast([P, P, PACK]),
+                    pw_of[k].unsqueeze(1).to_broadcast([P, P, PACK]),
                     ALU.mult,
                 )
                 return
@@ -237,7 +235,7 @@ def tile_list_region_patch_pool_kernel(
             else:
                 weighted = ring.tile([P, PACK, SLOT_PITCH], F32, name="weighted")
             for t in range(PACK):
-                nc.scalar.activation(weighted[:, t, 0:P], bank[:, t, :], ACT.Copy, scale=pw_half[k][t])
+                nc.scalar.activation(weighted[:, t, 0:P], bank[:, t, :], ACT.Copy, scale=pw_of[k][:, t : t + 1])
             nc.vector.scalar_tensor_tensor(
                 out=h_bf[b][:, c * PASS : (c + 1) * PASS].rearrange("p (j t) -> p j t", t=PACK),
                 in0=bank[:].rearrange("p t j -> p j t"),
@@ -285,6 +283,8 @@ def tile_list_region_patch_pool_kernel(
                 stop=True,
             )
         cast_x(0, 0)
+        own_weights(7, 2 * S2)
+        own_weights(11, S2)
         for k in range(EARLY_STEPS):
             score_pass(k, 0)
         gather_words(1, 0, 1)
@@ -298,15 +298,15 @@ def tile_list_region_patch_pool_kernel(
             score_pass(k, 1)
             make_h(k, on=V2_AT + 192 - 64 + 64 if k == 0 else None)
             if k == 7:
-                quantize_h(0, 0, JC, on="after_step7")
+                quantize_h(0, 0, JC, on=HOLD_AT)
                 quantize_h(1, 0, JC)
-                quantize_x(1, 0, NT, on="after_step7x")
+                quantize_x(1, 0, NT, on=HOLD_AT + S2)
                 cast_x(0, 3)
                 quantize_x(0, 0, NT)
             if k == 9:
                 cast_x(2, 0)
             if k == 11:
-                quantize_h(2, 1, 3, on="after_step11")
+                quantize_h(2, 1, 3, on=HOLD_AT + 2 * S2)
                 quantize_h(2, 0, 1)
                 quantize_h(2, 3, 4)
                 cast_x(2, 1)
@@ -339,7 +339,7 @@ def tile_list_region_patch_pool_kernel(
                     y_cols = sums[acc][:]
                 else:
                     y_cols = sums[("y", n), SUM_BANK["y"][n]][:, cols]
-                nc.scalar.activation(gate[:, cols], g_sum[:, cols], ACT.Tanh)
+                nc.scalar.activation(gate[:, cols], g_sum[:, cols], ACT.Tanh, scale=0.5)
                 nc.vector.scalar_tensor_tensor(
                     out=res[:, cols], in0=gate[:, cols], scalar=1.0, in1=y_cols, op0=ALU.add, op1=ALU.mult
                 )

@@ -25,8 +25,8 @@ LIST_COLS = PASS // 16
 SLOT_PITCH = P + 1
 
 WEIGHTED_BUFS = 4
-SCORE_BANK = [0, 1, 2, 3, 4, 5, 0, 1, 2, 3, 0, 1]
-SUM_BANK = {"g": [6, 7, 2, 0], "y": [4, 5, 3, 1]}
+SCORE_BANK = [0, 1, 2, 3, 4, 5, 6, 7, 0, 1, 2, 3]
+SUM_BANK = {"g": [4, 5, 0, 2], "y": [6, 7, 1, 3]}
 EARLY_STEPS = 2
 GPSIMD_STEP = 8
 CLEAR_SPLIT = 640
@@ -246,6 +246,7 @@ def tile_list_region_patch_pool_kernel(
             )
 
         sums = {}
+        last_sums = [(("y", NT - 1, h), (SUM_BANK["y"][NT - 1], SUM_BANK["g"][0], SUM_BANK["g"][1])[h]) for h in range(3)]
 
         def pool_pass(acc, kind, n, b, cols):
             if kind == "g":
@@ -284,7 +285,7 @@ def tile_list_region_patch_pool_kernel(
             )
         cast_x(0, 0)
         own_weights(7, 2 * S2)
-        own_weights(11, S2)
+        own_weights(11, 2 * S2)
         for k in range(EARLY_STEPS):
             score_pass(k, 0)
         gather_words(1, 0, 1)
@@ -300,7 +301,7 @@ def tile_list_region_patch_pool_kernel(
             if k == 7:
                 quantize_h(0, 0, JC, on=HOLD_AT)
                 quantize_h(1, 0, JC)
-                quantize_x(1, 0, NT, on=HOLD_AT + S2)
+                quantize_x(1, 0, 2, on=HOLD_AT + S2)
                 cast_x(0, 3)
                 quantize_x(0, 0, NT)
             if k == 9:
@@ -311,19 +312,22 @@ def tile_list_region_patch_pool_kernel(
                 quantize_h(2, 3, 4)
                 cast_x(2, 1)
                 quantize_x(2, 0, 2)
+                quantize_x(1, 2, NT, on=HOLD_AT + 3 * S2)
                 cast_x(2, 2)
                 cast_x(2, 3)
                 quantize_x(2, 2, 4)
-                for kind, order in (("g", (0, 1)), ("y", (1, 0))):
+                for kind, ns, order in (("g", (0, 1, 2), (0, 1)), ("y", (0, 1), (1, 0))):
                     for pb in order:
-                        for n in (0, 1):
+                        for n in ns:
                             pool(kind, n, pb)
-                for kind, n in (("g", 2), ("y", 2), ("g", 3)):
-                    for pb in (0, 1):
-                        pool(kind, n, pb)
+                for kind, n, pb in (("y", 2, 0), ("g", 3, 0), ("g", 3, 1)):
+                    pool(kind, n, pb)
+                pool_pass(last_sums[0], "y", NT - 1, 0, slice(0, 2 * P))
 
         for n in range(NT):
             pool("g", n, NB - 1)
+            if n == 2:
+                pool("y", n, 1)
             if n < NT - 1:
                 pool("y", n, NB - 1)
             g_sum = sums[("g", n), SUM_BANK["g"][n]]
@@ -333,8 +337,8 @@ def tile_list_region_patch_pool_kernel(
             for h in range(len(edges) - 1):
                 cols = slice(edges[h], edges[h + 1])
                 if n == NT - 1:
-                    acc = (("y", n, h), (SUM_BANK["y"][n], SUM_BANK["g"][0], SUM_BANK["g"][1])[h])
-                    for b in range(NB):
+                    acc = last_sums[h]
+                    for b in range(1 if h == 0 else 0, NB):
                         pool_pass(acc, "y", n, b, cols)
                     y_cols = sums[acc][:]
                 else:

@@ -29,6 +29,7 @@ SCORE_BANK = [0, 1, 2, 3, 4, 5, 6, 7, 0, 1, 2, 3]
 SUM_BANK = {"g": [4, 5, 0, 2], "y": [6, 7, 1, 3]}
 EARLY_STEPS = 2
 GPSIMD_STEP = 8
+CHUNKED = 1
 CLEAR_SPLIT = 640
 V2_AT = 4 * T + 6144 + 4096
 G4_AT = 0
@@ -135,9 +136,10 @@ def tile_list_region_patch_pool_kernel(
 
         pw_of = {k: pw_sb[:, k // JC, 0:PACK] for k in range(NB * JC)}
 
-        def own_weights(k, width):
-            pw_of[k] = tile(f"after_step{k}", [P, width // 4], F32, on=HOLD_AT + (k // 11) * 2 * S2)[:, 0:PACK]
-            nc.scalar.copy(pw_of[k], pw_sb[:, k // JC, 0:PACK])
+        halves = {}
+        for b, q, at in ((0, 3, HOLD_AT), (2, 1, HOLD_AT + 2 * S2)):
+            halves[b, q] = tile(f"half{b}", [P, S2 // 2], F32, on=at)[:, 0:1]
+            nc.gpsimd.memset(halves[b, q], 0.5)
 
         g4_sb = tile("g4_sb", [P, NB * 3 * N], U8, on=G4_AT)
         g4_w = g4_sb[:, 0 : NB * 2 * N].rearrange("p (b c) -> p b c", b=NB)
@@ -159,7 +161,7 @@ def tile_list_region_patch_pool_kernel(
             nc.scalar.mul(
                 x_bf[b][:, q * PASS : (q + 1) * PASS].rearrange("p (c i t) -> p c t i", i=4, t=PACK),
                 raw[:, :, at * P : (at + 1) * P].rearrange("p t (c i) -> p c t i", i=4),
-                0.5,
+                halves.get((b, q), 0.5),
             )
 
         def cast_x_gpsimd(b, q0, q1):
@@ -268,6 +270,18 @@ def tile_list_region_patch_pool_kernel(
                 stop=(b == NB - 1),
             )
 
+        def gate_chunk(n, c):
+            cols = slice(c * P, (c + 1) * P)
+            nc.tensor.matmul_mx(
+                out=sums[("g", n), SUM_BANK["g"][n]][:, cols],
+                lhsT=g4_w[:, NB - 1, 2 * n * P : 2 * (n + 1) * P].bitcast(E2M1),
+                lhsT_scale=g4_sc[:, NB - 1, n * P : (n + 1) * P],
+                rhs=h_w[NB - 1][:, cols].bitcast(E4M3),
+                rhs_scale=h_sc[NB - 1][:, cols],
+                start=False,
+                stop=(c == JC - 1),
+            )
+
         def pool(kind, n, b):
             pool_pass(((kind, n), SUM_BANK[kind][n]), kind, n, b, slice(0, S2))
 
@@ -284,8 +298,6 @@ def tile_list_region_patch_pool_kernel(
                 stop=True,
             )
         cast_x(0, 0)
-        own_weights(7, 2 * S2)
-        own_weights(11, 2 * S2)
         for k in range(EARLY_STEPS):
             score_pass(k, 0)
         gather_words(1, 0, 1)
@@ -299,18 +311,18 @@ def tile_list_region_patch_pool_kernel(
             score_pass(k, 1)
             make_h(k, on=V2_AT + 192 - 64 + 64 if k == 0 else None)
             if k == 7:
+                cast_x(0, 3)
                 quantize_h(0, 0, JC, on=HOLD_AT)
                 quantize_h(1, 0, JC)
                 quantize_x(1, 0, 2, on=HOLD_AT + S2)
-                cast_x(0, 3)
                 quantize_x(0, 0, NT)
             if k == 9:
                 cast_x(2, 0)
             if k == 11:
+                cast_x(2, 1)
                 quantize_h(2, 1, 3, on=HOLD_AT + 2 * S2)
                 quantize_h(2, 0, 1)
                 quantize_h(2, 3, 4)
-                cast_x(2, 1)
                 quantize_x(2, 0, 2)
                 quantize_x(1, 2, NT, on=HOLD_AT + 3 * S2)
                 cast_x(2, 2)
@@ -324,8 +336,14 @@ def tile_list_region_patch_pool_kernel(
                     pool(kind, n, pb)
                 pool_pass(last_sums[0], "y", NT - 1, 0, slice(0, 2 * P))
 
+        for c in (1, 2, 0):
+            for n in range(CHUNKED):
+                gate_chunk(n, c)
         for n in range(NT):
-            pool("g", n, NB - 1)
+            if n < CHUNKED:
+                gate_chunk(n, JC - 1)
+            else:
+                pool("g", n, NB - 1)
             if n == 2:
                 pool("y", n, 1)
             if n < NT - 1:

@@ -128,8 +128,10 @@ def tile_list_region_patch_pool_kernel(
         gather_small(1)
         load_x(0, 0, 1, on=V2_AT + 192)
         pw_sb = tile("pw_sb", [P, NB, 8], F32, on=V2_AT + 64)
-        nc.sync.dma_start(pw_sb[:, :, 0:PACK], pw.rearrange("(b p t) -> p b t", p=P, t=PACK))
+        pw_rows = pw.rearrange("(b p t) -> p b t", p=P, t=PACK)
+        nc.sync.dma_start(pw_sb[:, 0, 0:PACK], pw_rows[:, 0, :])
         load_x(1, 0, 4, on=V2_AT + 192 + 2112)
+        nc.sync.dma_start(pw_sb[:, 1:NB, 0:PACK], pw_rows[:, 1:NB, :])
         load_x(0, 1, 4, on=V2_AT + 64 - 6144)
         gather_words(0, 0, 1)
         gather_words(0, 1, NB)

@@ -139,7 +139,7 @@ def tile_list_region_patch_pool_kernel(
         pw_of = {k: pw_sb[:, k // JC, 0:PACK] for k in range(NB * JC)}
 
         halves = {}
-        for b, q, at in ((0, 3, HOLD_AT), (2, 1, HOLD_AT + 2 * S2)):
+        for b, q, at in ((0, 3, HOLD_AT), (2, 0, HOLD_AT + 2 * S2)):
             halves[b, q] = tile(f"half{b}", [P, S2 // 2], F32, on=at)[:, 0:1]
             nc.gpsimd.memset(halves[b, q], 0.5)
 
@@ -318,13 +318,12 @@ def tile_list_region_patch_pool_kernel(
                 quantize_h(1, 0, JC)
                 quantize_x(1, 0, 2, on=HOLD_AT + S2)
                 quantize_x(0, 0, NT)
-            if k == 9:
-                cast_x(2, 0)
             if k == 11:
-                cast_x(2, 1)
+                cast_x(2, 0)
                 quantize_h(2, 1, 3, on=HOLD_AT + 2 * S2)
                 quantize_h(2, 0, 1)
                 quantize_h(2, 3, 4)
+                cast_x(2, 1)
                 quantize_x(2, 0, 2)
                 quantize_x(1, 2, NT, on=HOLD_AT + 3 * S2)
                 cast_x(2, 2)

from contextlib import ExitStack

import concourse.mybir as mybir

F32 = mybir.dt.float32
BF16 = mybir.dt.bfloat16
I32 = mybir.dt.int32
U32 = mybir.dt.uint32
U16 = mybir.dt.uint16
U8 = mybir.dt.uint8
E4M3 = mybir.dt.float8_e4m3fn_x4
E2M1 = mybir.dt.float4_e2m1fn_x4
ALU = mybir.AluOpType
ACT = mybir.ActivationFunctionType

P = 128
K, T, S, T2, S2, N = 1024, 4096, 1536, 1024, 512, 512
PACK = 4
PASS = P * PACK
KP = K // PASS
NB = S // PASS
JC = S2 // P
NT = N // P
LIST_COLS = PASS // 16
SLOT_PITCH = P + 1

WEIGHTED_BUFS = 4
SCORE_BANK = [0, 1, 2, 3, 4, 5, 6, 7, 0, 1, 2, 3]
SUM_BANK = {"g": [4, 5, 0, 2], "y": [6, 7, 1, 3]}
EARLY_STEPS = 2
GPSIMD_STEP = 8
CHUNKED = 1
CLEAR_SPLIT = 640
V2_AT = 4 * T + 6144 + 4096
G4_AT = 0
HOLD_AT = V2_AT + 16384
GP_STEPS = (8,)

FLOPS = 2 * K * S * S2 + 2 * 2 * S * N * S2


def tile_list_region_patch_pool_kernel(
    tc, tab_words, tab_scales, offs, tab2_words, tab2_scales, offs2, pw, x, g4_words, g4_scales, out
):
    nc = tc.nc
    with ExitStack() as ctx:
        keep = ctx.enter_context(tc.tile_pool(name="keep", bufs=1))
        ring = ctx.enter_context(tc.tile_pool(name="ring", bufs=WEIGHTED_BUFS))
        psum = ctx.enter_context(tc.psum_pool(name="psum", bufs=1))

        shared = ctx.enter_context(tc.tile_pool(name="shared", bufs=1))

        def tile(name, shape, dtype, on=None):
            if isinstance(on, int):
                return shared.tile(shape, dtype, name=name, offset=on, align_bytes=64)
            return keep.tile(shape, dtype, name=name, tag=on or name, align_bytes=64)

        idx = keep.tile([P, S // 16], U16, name="idx")
        idx2 = keep.tile([P, S2 // 16], U16, name="idx2")
        v_tab = [tile(f"v_tab{a}", [P, T], I32, on=0 if a == 0 else None) for a in range(KP)]
        v2_tab = [tile(f"v2_tab{a}", [P, T2], I32, on=V2_AT if a == 1 else None) for a in range(KP)]
        v_tab_sc = tile("v_tab_sc", [P, T // 4], I32)
        v2_tab_sc = tile("v2_tab_sc", [P, T2 // 4], I32)

        nc.gpsimd.memset(v2_tab_sc[:], 0)
        nc.vector.memset(v_tab_sc[:, 0:CLEAR_SPLIT], 0)
        nc.gpsimd.memset(v_tab_sc[:, CLEAR_SPLIT:], 0)

        def words_of(table, a):
            return table[a].rearrange("p t i -> p (t i)").bitcast(I32)

        def spread_rows(scales):
            return scales.rearrange("a r c -> r a c").bitcast(I32)

        x_raw = {}

        def load_x(b, q0, q1, on=None):
            raw = tile(f"x_raw{b}_{q0}", [P, PACK, (q1 - q0) * P], F32, on)
            rows = x[b * PASS : (b + 1) * PASS, :].rearrange("(p t) n -> p t n", t=PACK)
            nc.sync.dma_start(raw[:], rows[:, :, q0 * P : q1 * P])
            for q in range(q0, q1):
                x_raw[b, q] = (raw, q - q0)

        nc.sync.dma_start(idx2[:], offs2)
        nc.sync.dma_start(idx[:], offs)
        nc.sync.dma_start(v2_tab_sc[0:P:4, :], spread_rows(tab2_scales))
        nc.sync.dma_start(v2_tab[0][:], words_of(tab2_words, 0))
        nc.sync.dma_start(v_tab_sc[0:P:4, :], spread_rows(tab_scales))
        nc.sync.dma_start(v2_tab[1][:], words_of(tab2_words, 1))
        nc.sync.dma_start(v_tab[0][:], words_of(tab_words, 0))

        nc.sync.dma_start(v_tab[1][:], words_of(tab_words, 1))

        v2_w = [tile(f"v2_w{a}", [P, S2], U32) for a in range(KP)]
        v_w = [tile(f"v_w{a}", [P, S], U32) for a in range(KP)]
        v2_sc_list = tile("v2_sc_list", [P, S2], U8)
        v_sc_list = tile("v_sc_list", [P, S], U8)
        tab_sc = tile("tab_sc", [P, S + S2], U8)

        def gather_small(a):
            nc.vector.tensor_copy(v2_w[a][:], v2_tab[a][:].bitcast(U32).indirect(idx2[:]))

        def gather_words(a, b0, b1):
            nc.vector.tensor_copy(
                v_w[a][:, b0 * PASS : b1 * PASS].rearrange("p (b t m) -> p b m t", t=PACK, m=P),
                v_tab[a][:].bitcast(U32).indirect(idx[:, b0 * LIST_COLS : b1 * LIST_COLS]),
            )

        nc.vector.tensor_copy(v2_sc_list[:], v2_tab_sc[:].bitcast(U8).indirect(idx2[:]))
        gather_small(0)
        parts = ((0, NB - 1), (NB - 1, NB))
        for b0, b1 in parts:
            nc.vector.tensor_copy(
                v_sc_list[:, b0 * PASS : b1 * PASS],
                v_tab_sc[:].bitcast(U8).indirect(idx[:, b0 * LIST_COLS : b1 * LIST_COLS]),
            )
        for b0, b1 in parts:
            nc.vector.tensor_copy(
                tab_sc[:, b0 * PASS : b1 * PASS].rearrange("p (b t m) -> p t b m", t=PACK, m=P),
                v_sc_list[:, b0 * PASS : b1 * PASS].rearrange("p (b m t) -> p t b m", t=PACK, m=P),
            )
        nc.vector.tensor_copy(tab_sc[:, S:].bitcast(I32), v2_sc_list[:].bitcast(I32))
        for a in range(KP):
            for r in range(1, 4):
                nc.sync.dma_start(
                    tab_sc[4 * a + r : P : 32, :].bitcast(I32), tab_sc[4 * a + 8 * r : P : 32, :].bitcast(I32)
                )
        gather_small(1)
        load_x(0, 0, 1, on=V2_AT + 192)
        pw_sb = tile("pw_sb", [P, NB, 8], F32, on=V2_AT + 64)
        pw_rows = pw.rearrange("(b p t) -> p b t", p=P, t=PACK)
        nc.sync.dma_start(pw_sb[:, 0, 0:PACK], pw_rows[:, 0, :])
        load_x(1, 0, 4, on=V2_AT + 192 + 2112)
        nc.sync.dma_start(pw_sb[:, 1:NB, 0:PACK], pw_rows[:, 1:NB, :])
        load_x(0, 1, 4, on=V2_AT + 64 - 6144)
        gather_words(0, 0, 1)
        gather_words(0, 1, NB)

        pw_of = {k: pw_sb[:, k // JC, 0:PACK] for k in range(NB * JC)}

        halves = {}
        for b, q, at in ((0, 3, HOLD_AT), (2, 0, HOLD_AT + 2 * S2)):
            halves[b, q] = tile(f"half{b}", [P, S2 // 2], F32, on=at)[:, 0:1]
            nc.gpsimd.memset(halves[b, q], 0.5)

        g4_sb = tile("g4_sb", [P, NB * 3 * N], U8, on=G4_AT)
        g4_w = g4_sb[:, 0 : NB * 2 * N].rearrange("p (b c) -> p b c", b=NB)
        g4_sc = g4_sb[:, NB * 2 * N :].rearrange("p (b c) -> p b c", b=NB)
        for q in range(4):
            nc.sync.dma_start(
                g4_sc[32 * q : 32 * q + 4, :, :].bitcast(I32), spread_rows(g4_scales[:, 4 * q : 4 * q + 4, :])
            )
        nc.sync.dma_start(g4_w.bitcast(I32), g4_words.rearrange("a p c -> p a c").bitcast(I32))

        x_bf = [tile(f"x_bf{b}", [P, N * PACK], BF16, on="v_tab1" if b == 1 else None) for b in range(NB)]
        x_w = [tile(f"x_w{b}", [P, N], U32) for b in range(NB)]
        h_bf = [tile(f"h_bf{b}", [P, S2 * PACK], BF16) for b in range(NB)]
        h_w = [tile(f"h_w{b}", [P, S2], U32) for b in range(NB)]
        x_sc, h_sc, h_gpsimd = {}, {}, []

        def cast_x(b, q):
            raw, at = x_raw[b, q]
            nc.scalar.mul(
                x_bf[b][:, q * PASS : (q + 1) * PASS].rearrange("p (c i t) -> p c t i", i=4, t=PACK),
                raw[:, :, at * P : (at + 1) * P].rearrange("p t (c i) -> p c t i", i=4),
                halves.get((b, q), 0.5),
            )

        def cast_x_gpsimd(b, q0, q1):
            raw, at = x_raw[b, q0]
            nc.gpsimd.tensor_scalar(
                x_bf[b][:, q0 * PASS : q1 * PASS].rearrange("p (j t) -> p j t", t=PACK),
                raw[:, :, at * P : (at + q1 - q0) * P].rearrange("p t j -> p j t"),
                0.5,
                0.0,
                ALU.mult,
                ALU.add,
            )

        def quantize_x(b, n0, n1, on=None):
            scales = tile(f"x_sc{b}_{n0}", [P, (n1 - n0) * P], U8, on)
            for n in range(n0, n1):
                x_sc[b, n] = scales[:, (n - n0) * P : (n - n0 + 1) * P]
            nc.vector.quantize_mx(
                out=x_w[b][:, n0 * P : n1 * P].bitcast(E4M3), scales=scales[:], in_=x_bf[b][:, n0 * PASS : n1 * PASS]
            )

        def quantize_h(b, c0, c1, on=None):
            if b not in h_sc:
                h_sc[b] = tile(f"h_sc{b}", [P, S2], U8, on)
            nc.vector.quantize_mx(
                out=h_w[b][:, c0 * P : c1 * P].bitcast(E4M3),
                scales=h_sc[b][:, c0 * P : c1 * P],
                in_=h_gpsimd[0][:] if b * JC + c0 == GPSIMD_STEP else h_bf[b][:, c0 * PASS : c1 * PASS],
            )

        banks = {}

        def score_pass(k, a):
            b, c = divmod(k, JC)
            if a == 0:
                banks[k] = psum.tile([P, PACK, P], F32, name="bank", tag=f"bank{SCORE_BANK[k]}")
            for t in range(PACK):
                slot = slice(b * PASS + t * P, b * PASS + (t + 1) * P)
                nc.tensor.matmul_mx(
                    out=banks[k][:, t, :],
                    lhsT=v_w[a][:, slot].bitcast(E4M3),
                    lhsT_scale=tab_sc[4 * a :, slot],
                    rhs=v2_w[a][:, c * P : (c + 1) * P].bitcast(E4M3),
                    rhs_scale=tab_sc[4 * a :, S + c * P : S + (c + 1) * P],
                    start=(a == 0 and t == 0),
                    stop=(a == KP - 1 and t == PACK - 1),
                )

        def make_h(k, on=None):
            b, c = divmod(k, JC)
            bank = banks[k]
            if k in GP_STEPS:
                kept = tile(f"kept{k}", [P, PASS], F32, on)
                squared = tile(f"squared{k}", [P, PASS], F32)
                nc.scalar.activation(
                    kept[:].rearrange("p (j t) -> p j t", t=PACK), bank[:].rearrange("p t j -> p j t"), ACT.Relu
                )
                nc.scalar.activation(squared[:], kept[:], ACT.Square)
                if k == GPSIMD_STEP:
                    h_gpsimd.append(tile("h_gpsimd", [P, PASS], BF16, on="x_bf0"))
                    h_out = h_gpsimd[0][:]
                else:
                    h_out = h_bf[b][:, c * PASS : (c + 1) * PASS]
                nc.gpsimd.tensor_tensor(
                    h_out.rearrange("p (j t) -> p j t", t=PACK),
                    squared[:].rearrange("p (j t) -> p j t", t=PACK),
                    pw_of[k].unsqueeze(1).to_broadcast([P, P, PACK]),
                    ALU.mult,
                )
                return
            if on is not None:
                weighted = tile(f"weighted{k}", [P, PACK, SLOT_PITCH], F32, on)
            else:
                weighted = ring.tile([P, PACK, SLOT_PITCH], F32, name="weighted")
            for t in range(PACK):
                nc.scalar.activation(weighted[:, t, 0:P], bank[:, t, :], ACT.Copy, scale=pw_of[k][:, t : t + 1])
            nc.vector.scalar_tensor_tensor(
                out=h_bf[b][:, c * PASS : (c + 1) * PASS].rearrange("p (j t) -> p j t", t=PACK),
                in0=bank[:].rearrange("p t j -> p j t"),
                scalar=0.0,
                in1=weighted[:, :, 0:P].rearrange("p t j -> p j t"),
                op0=ALU.max,
                op1=ALU.mult,
            )

        sums = {}
        last_sums = [(("y", NT - 1, h), (SUM_BANK["y"][NT - 1], SUM_BANK["g"][0], SUM_BANK["g"][1])[h]) for h in range(3)]

        def pool_pass(acc, kind, n, b, cols):
            if kind == "g":
                lhsT = g4_w[:, b, 2 * n * P : 2 * (n + 1) * P].bitcast(E2M1)
                lhsT_scale = g4_sc[:, b, n * P : (n + 1) * P]
            else:
                lhsT = x_w[b][:, n * P : (n + 1) * P].bitcast(E4M3)
                lhsT_scale = x_sc[b, n]
            first = acc not in sums
            if first:
                sums[acc] = psum.tile([P, cols.stop - cols.start], F32, name="sum", tag=f"bank{acc[1]}")
            nc.tensor.matmul_mx(
                out=sums[acc][:],
                lhsT=lhsT,
                lhsT_scale=lhsT_scale,
                rhs=h_w[b][:, cols].bitcast(E4M3),
                rhs_scale=h_sc[b][:, cols],
                start=first,
                stop=(b == NB - 1),
            )

        def gate_chunk(n, c):
            cols = slice(c * P, (c + 1) * P)
            nc.tensor.matmul_mx(
                out=sums[("g", n), SUM_BANK["g"][n]][:, cols],
                lhsT=g4_w[:, NB - 1, 2 * n * P : 2 * (n + 1) * P].bitcast(E2M1),
                lhsT_scale=g4_sc[:, NB - 1, n * P : (n + 1) * P],
                rhs=h_w[NB - 1][:, cols].bitcast(E4M3),
                rhs_scale=h_sc[NB - 1][:, cols],
                start=False,
                stop=(c == JC - 1),
            )

        def pool(kind, n, b):
            pool_pass(((kind, n), SUM_BANK[kind][n]), kind, n, b, slice(0, S2))

        load_x(2, 0, NT, on=G4_AT + 4608)
        warm = psum.tile([P, PASS], F32, name="warm", tag="bank7")
        for w in range(4):
            nc.tensor.matmul_mx(
                out=warm[:],
                lhsT=v2_w[0][:, w * P : (w + 1) * P].bitcast(E4M3),
                lhsT_scale=v2_sc_list[:, w * P : (w + 1) * P],
                rhs=v_w[0][:, 0:PASS].bitcast(E4M3),
                rhs_scale=v_sc_list[:, 0:PASS],
                start=True,
                stop=True,
            )
        cast_x(0, 0)
        for k in range(EARLY_STEPS):
            score_pass(k, 0)
        gather_words(1, 0, 1)
        gather_words(1, 1, NB)
        cast_x_gpsimd(1, 0, 2)
        cast_x_gpsimd(0, 1, 3)
        cast_x_gpsimd(1, 2, 4)
        for k in range(NB * JC):
            if k >= EARLY_STEPS:
                score_pass(k, 0)
            score_pass(k, 1)
            make_h(k, on=V2_AT + 192 - 64 + 64 if k == 0 else None)
            if k == 7:
                cast_x(0, 3)
                quantize_h(0, 0, JC, on=HOLD_AT)
                quantize_h(1, 0, JC)
                quantize_x(1, 0, 2, on=HOLD_AT + S2)
                quantize_x(0, 0, NT)
            if k == 11:
                cast_x(2, 0)
                quantize_h(2, 1, 3, on=HOLD_AT + 2 * S2)
                quantize_h(2, 0, 1)
                quantize_h(2, 3, 4)
                cast_x(2, 1)
                quantize_x(2, 0, 2)
                quantize_x(1, 2, NT, on=HOLD_AT + 3 * S2)
                cast_x(2, 2)
                cast_x(2, 3)
                quantize_x(2, 2, 4)
                for kind, ns, order in (("g", (0, 1, 2), (0, 1)), ("y", (0, 1), (1, 0))):
                    for pb in order:
                        for n in ns:
                            pool(kind, n, pb)
                for kind, n, pb in (("y", 2, 0), ("g", 3, 0), ("g", 3, 1)):
                    pool(kind, n, pb)
                pool_pass(last_sums[0], "y", NT - 1, 0, slice(0, 2 * P))

        for c in (1, 2, 0):
            for n in range(CHUNKED):
                gate_chunk(n, c)
        for n in range(NT):
            if n < CHUNKED:
                gate_chunk(n, JC - 1)
            else:
                pool("g", n, NB - 1)
            if n == 2:
                pool("y", n, 1)
            if n < NT - 1:
                pool("y", n, NB - 1)
            g_sum = sums[("g", n), SUM_BANK["g"][n]]
            gate = keep.tile([P, S2], F32, name=f"gate{n}")
            res = keep.tile([P, S2], F32, name=f"res{n}")
            edges = (0, 2 * P, 3 * P, S2) if n == NT - 1 else (0, 2 * P, S2)
            for h in range(len(edges) - 1):
                cols = slice(edges[h], edges[h + 1])
                if n == NT - 1:
                    acc = last_sums[h]
                    for b in range(1 if h == 0 else 0, NB):
                        pool_pass(acc, "y", n, b, cols)
                    y_cols = sums[acc][:]
                else:
                    y_cols = sums[("y", n), SUM_BANK["y"][n]][:, cols]
                nc.scalar.activation(gate[:, cols], g_sum[:, cols], ACT.Tanh, scale=0.5)
                nc.vector.scalar_tensor_tensor(
                    out=res[:, cols], in0=gate[:, cols], scalar=1.0, in1=y_cols, op0=ALU.add, op1=ALU.mult
                )
                if n in (0, NT - 1):
                    nc.sync.dma_start(out[n * P : (n + 1) * P, cols], res[:, cols])
            if 0 < n < NT - 1:
                nc.sync.dma_start(out[n * P : (n + 1) * P, :], res[:])
